import numpy as np
import ml_dtypes


def mxq(x, axis, fmt="e4m3"):
    dtype, down = {"e4m3": (ml_dtypes.float8_e4m3fn, 7), "e5m2": (ml_dtypes.float8_e5m2, 14)}[fmt]
    v = np.moveaxis(np.asarray(x, np.float32).astype(ml_dtypes.bfloat16).astype(np.float64), axis, -1)
    blocks = v.reshape(v.shape[:-1] + (-1, 32))
    amax = np.abs(blocks).max(-1, keepdims=True)
    byte = np.maximum(np.where(amax > 0, np.frexp(amax)[1] - 1 + 127, 0) - down, 1)
    scale = np.exp2(byte - 127.0)
    codes = (blocks / scale).astype(np.float32).astype(dtype).astype(np.float64)
    return np.moveaxis((codes * scale).reshape(v.shape), -1, axis)


WIDE = False


def mx_kscale(k):
    if not WIDE:
        return np.ones(k)
    levels = np.array([10, -10, 5, -5, 0])
    if k % 512:
        return np.exp2(np.random.permutation(np.resize(levels, k // 32))).repeat(32)
    a = np.empty((k // 512, 16))
    for p in range(k // 512):
        a[p, :8] = np.random.permutation(np.resize(levels, 8))
        for g in range(8):
            far = levels[np.abs(levels - a[p, g]) >= 10]
            a[p, g + 8] = far[np.random.randint(len(far))]
    return np.exp2(a.ravel()).repeat(32)


def f64(x):
    return np.asarray(x).astype(np.float64)


def striped(idx):
    return np.tile(idx.reshape(-1, 16).T, (8, 1)).astype(np.uint16)


def unstriped(offs):
    return offs[:16].T.reshape(-1).astype(np.int64)


def pack_weight(w):
    k, n = w.shape
    w = f64(np.asarray(w, np.float32).astype(ml_dtypes.bfloat16)).reshape(k // 32, 32, n)
    amax = np.abs(w).max(1)
    byte = np.clip(np.where(amax > 0, np.frexp(amax)[1] - 1 + 127 - 7, 1), 1, 254)
    scaled = (w * np.exp2(127.0 - byte)[:, None, :]).reshape(k, n).astype(np.float32)
    words = np.ascontiguousarray(scaled.reshape(k // 512, 128, 4, n).transpose(0, 1, 3, 2)).astype(ml_dtypes.float8_e4m3fn).view(np.uint8)
    return words, np.ascontiguousarray(byte.astype(np.uint8).reshape(k // 512, 16, n))


def unpack_weight(words, scales):
    g, p, n, _ = words.shape
    vals = np.ascontiguousarray(words).view(ml_dtypes.float8_e4m3fn).astype(np.float64) * np.repeat(np.exp2(scales.astype(np.float64) - 127.0), 8, axis=1)[..., None]
    return vals.transpose(0, 1, 3, 2).reshape(g * 512, n)


K, T, E, C, N = 1024, 768, 6, 128, 128
M = 1024


def by_expert(wq, xq):
    return np.concatenate([wq[e].T @ xq[:, e * C:(e + 1) * C] for e in range(E)], axis=1)


def setup_inputs():
    n = np.random.standard_normal
    s = mx_kscale(K)[:, None]
    packed = [pack_weight(m) for m in n((E, K, N)) / np.sqrt(K) / s[None]]
    r = mx_kscale(M)[:, None]
    return {
        "uT": (n((M, T)) * r).astype(np.float32),
        "wu": (n((M, K)) / np.sqrt(M) / r * s.T).astype(np.float32),
        "w_words": np.stack([m[0] for m in packed]),
        "w_scales": np.stack([m[1] for m in packed]),
        "b": (0.3 * n((N, E))).astype(np.float32),
        "gate": np.tile(np.random.uniform(0.2, 1.0, E * C), (N, 1)).astype(np.float32),
        "offs": striped(np.random.permutation(T)[:E * C]),
    }


def reference(uT, wu, w_words, w_scales, b, gate, offs):
    idx = unstriped(offs)
    w = np.stack([unpack_weight(w_words[e], w_scales[e]) for e in range(E)])
    x = mxq(f64(wu), 0, "e4m3").T @ mxq(f64(uT), 0, "e4m3")
    xq = mxq(x[:, idx], 0, "e4m3")
    y = by_expert(w, xq)
    y = y + np.repeat(f64(b), C, axis=1)
    out = np.zeros((N, T))
    out[:, idx] = f64(gate) * y
    return out

@@ -1,0 +1,265 @@
+from contextlib import ExitStack
+
+import concourse.mybir as mybir
+
+M, K, T, E, C, N = 1024, 1024, 768, 6, 128, 128
+FLOPS = 2 * M * K * T + 2 * K * N * E * C
+
+F32 = mybir.dt.float32
+BF16 = mybir.dt.bfloat16
+I32 = mybir.dt.int32
+U32 = mybir.dt.uint32
+U16 = mybir.dt.uint16
+U8 = mybir.dt.uint8
+FP8X4 = mybir.dt.float8_e4m3fn_x4
+IDENTITY = mybir.ActivationFunctionType.Identity
+MULT = mybir.AluOpType.mult
+
+P = 128
+PACK = 4
+PASS = P * PACK
+PASSES = 2
+S = E * C
+PER_COLUMN = 16
+BANKS = ((0, 1, 2, 3, 0, 1), (4, 5, 6, 7, 2, 3))
+
+
+def tile_moe_prv_lin_bias_kernel(tc, uT, wu, w_words, w_scales, b, gate, offs, out):
+    nc = tc.nc
+    with ExitStack() as ctx:
+        keep = ctx.enter_context(tc.tile_pool(name="keep", bufs=1))
+        shared = ctx.enter_context(tc.tile_pool(name="shared", bufs=1))
+        psum = ctx.enter_context(tc.psum_pool(name="psum", bufs=1))
+        banks = [psum.tile([P, PACK, C], F32, name="bank%d" % i) for i in range(8)]
+
+        def bank_of(a, e):
+            return banks[BANKS[a][e]]
+
+        offsets = keep.tile([P, S // PER_COLUMN], U16, name="offsets")
+
+        def slots(first, count):
+            return offsets[:, first // PER_COLUMN : (first + count) // PER_COLUMN]
+
+        u_rows = uT.rearrange("(g p h i) t -> g h p i t", g=PASSES, p=P, h=2)
+        u_raw = {}
+        for g in range(PASSES):
+            for h in range(2):
+                u_raw[g, h] = keep.tile([P, 2, T], F32, name="u_raw%d%d" % (g, h))
+                nc.sync.dma_start(out=u_raw[g, h][:], in_=u_rows[g, h])
+                if (g, h) == (0, 0):
+                    nc.sync.dma_start(offsets[:], offs)
+        wu_rows = wu.rearrange("(g p j) (a c) -> g a p j c", g=PASSES, p=P, a=PASSES)
+        wu_raw = {}
+        for a in range(PASSES):
+            for g in range(PASSES):
+                if (g, a) == (1, 1):
+                    wu_raw[g, a] = shared.tile([P, PACK, PASS], F32, name="wu_raw11", offset=0, align_bytes=64)
+                else:
+                    wu_raw[g, a] = keep.tile([P, PACK, PASS], F32, name="wu_raw%d%d" % (g, a))
+                nc.sync.dma_start(out=wu_raw[g, a][:], in_=wu_rows[g, a])
+        w_codes = keep.tile([P, E * PASSES, N * PACK], U8, name="w_codes", align_bytes=64)
+        w_src = w_words.rearrange("e a p n r -> p (e a) (n r)")
+
+        def load_w(half):
+            part = slice(half * E, (half + 1) * E)
+            nc.sync.dma_start(out=w_codes[:, part, :].bitcast(I32), in_=w_src[:, part, :].bitcast(I32))
+
+        load_w(0)
+        w_scale = keep.tile([P, E * PASSES, N], U8, name="w_scale", align_bytes=64)
+        nc.gpsimd.memset(w_scale[:].bitcast(I32), 0)
+        scale_src = w_scales.rearrange("e a q n -> q (e a) n")
+        for quad in range(4):
+            nc.sync.dma_start(
+                out=w_scale[32 * quad : 32 * quad + 4, :, :].bitcast(I32),
+                in_=scale_src[4 * quad : 4 * quad + 4].bitcast(I32),
+            )
+        bias = keep.tile([P, E], F32, name="bias")
+        nc.sync.dma_start(out=bias[:], in_=b)
+        gate_sb = keep.tile([P, S], F32, name="gate_sb")
+        nc.sync.dma_start(out=gate_sb[:], in_=gate)
+        load_w(1)
+
+        u_codes = keep.tile([P, PASSES, S], U32, name="u_codes", align_bytes=64)
+        u_scale = keep.tile([P, PASSES, S], U8, name="u_scale", align_bytes=64)
+        wu_grouped = keep.tile([P, 3, PASS * PACK], BF16, name="wu_grouped", align_bytes=64)
+        windows = {}
+
+        def round_pairs(g, h):
+            pairs = keep.tile([P, T, 2], BF16, name="pairs%d%d" % (g, h))
+            src = u_raw[g, h][:].rearrange("p i t -> p t i")
+            if g == 0:
+                cut = (512, 256)[h]
+                nc.scalar.activation(pairs[:, cut:, :], src[:, cut:, :], IDENTITY)
+                nc.vector.tensor_copy(out=pairs[:, :cut, :], in_=src[:, :cut, :])
+            else:
+                nc.scalar.copy(out=pairs[:], in_=src)
+            windows[g, h] = pairs[:].rearrange("p t i -> p (t i)").bitcast(U32)
+
+        def gather(g, h, cut, picked):
+            nc.vector.tensor_copy(out=picked[:, h, :], in_=windows[g, h].indirect(slots(cut.start, cut.stop - cut.start)))
+
+        u_grouped = keep.tile([P, PASSES, S * PACK], BF16, name="u_grouped", align_bytes=64)
+
+        def interleave(stage, picked):
+            nc.vector.tensor_copy(
+                out=stage.rearrange("p (s h i) -> p s h i", h=2, i=2),
+                in_=picked.bitcast(BF16).rearrange("p h (s i) -> p s h i", i=2),
+            )
+
+        def quantise_u(g, cut, stage):
+            nc.vector.quantize_mx(
+                out=u_codes[:, g, cut].bitcast(FP8X4),
+                scales=u_scale[:, g, cut],
+                in_=stage,
+            )
+
+        early, late = slice(0, 512), slice(512, S)
+        picked0 = keep.tile([P, 2, S], U32, name="picked0")
+        for h in range(2):
+            round_pairs(0, h)
+            for cut in (early, late):
+                gather(0, h, cut, picked0[:, :, cut])
+
+        def u_stage(g, cut):
+            return u_grouped[:, g, cut.start * PACK : cut.stop * PACK]
+
+        for cut in (early, late):
+            interleave(u_stage(0, cut), picked0[:, :, cut])
+        for cut in (early, late):
+            quantise_u(0, cut, u_stage(0, cut))
+        picked1 = keep.tile([P, 2, 512], U32, name="picked1")
+        picked_late = shared.tile([P, 2, 256], U32, name="picked_late", offset=1024, align_bytes=64)
+        for h in range(2):
+            round_pairs(1, h)
+            gather(1, h, early, picked1[:])
+        interleave(u_stage(1, early), picked1[:])
+
+        wu_codes = keep.tile([P, PASSES, PASSES, PASS], U32, name="wu_codes", align_bytes=64)
+        wu_scale = keep.tile([P, PASSES, PASSES, PASS], U8, name="wu_scale", align_bytes=64)
+        vector_share = {(0, 0): 0, (1, 0): 0, (0, 1): 40, (1, 1): P}
+
+        def wu_stage(g, a):
+            return wu_grouped[:, min(2 * a + g, 2), :]
+
+        def round_wu(g, a):
+            dst = wu_stage(g, a).rearrange("p (r m j) -> p m j r", r=PACK, j=PACK)
+            src = wu_raw[g, a][:].rearrange("p j (m r) -> p m j r", r=PACK)
+            cut = vector_share[g, a]
+            if cut > 0:
+                nc.vector.tensor_copy(out=dst[:, :cut], in_=src[:, :cut])
+            if cut < P:
+                nc.scalar.copy(out=dst[:, cut:], in_=src[:, cut:])
+
+        def quantise_wu(g, a):
+            nc.vector.quantize_mx(
+                out=wu_codes[:, g, a, :].bitcast(FP8X4), scales=wu_scale[:, g, a, :], in_=wu_stage(g, a)
+            )
+
+        x_grouped = keep.tile([P, PASSES, S * PACK], BF16, name="x_grouped", align_bytes=64)
+        late_stage = keep.tile([P, 2 * C * PACK], BF16, name="late_stage", align_bytes=64)
+        x_codes = keep.tile([P, PASSES, S], U32, name="x_codes", align_bytes=64)
+        x_scale = [
+            shared.tile([P, S], U8, name="x_scale0", offset=0, align_bytes=64),
+            keep.tile([P, S], U8, name="x_scale1", align_bytes=64),
+        ]
+
+        def x_stage(a, first, count):
+            if (a, first) == (1, 0):
+                return late_stage[:, : C * PACK]
+            return x_grouped[:, a, first * C * PACK : (first + count) * C * PACK]
+
+        def project(a, e):
+            cols = slice(e * C, (e + 1) * C)
+            bank = bank_of(a, e)
+            for r in range(PACK):
+                for g in range(PASSES):
+                    nc.tensor.matmul_mx(
+                        out=bank[:, r, :],
+                        lhsT=wu_codes[:, g, a, r * P : (r + 1) * P].bitcast(FP8X4),
+                        lhsT_scale=wu_scale[:, g, a, r * P : (r + 1) * P],
+                        rhs=u_codes[:, g, cols].bitcast(FP8X4),
+                        rhs_scale=u_scale[:, g, cols],
+                        start=(g == 0),
+                        stop=(g == PASSES - 1),
+                    )
+            nc.scalar.copy(out=x_stage(a, e, 1).rearrange("p (s r) -> p s r", r=PACK), in_=bank[:].rearrange("p r s -> p s r"))
+
+        def quantise_x(a, first, count):
+            cols = slice(first * C, (first + count) * C)
+            nc.vector.quantize_mx(
+                out=x_codes[:, a, cols].bitcast(FP8X4), scales=x_scale[a][:, cols], in_=x_stage(a, first, count)
+            )
+
+        y_own = keep.tile([P, S], F32, name="y_own")
+
+        def y(first, count):
+            if first == 3:
+                return x_stage(1, 4, 1).bitcast(F32)[:, :C]
+            return y_own[:, first * C : (first + count) * C]
+
+        result = keep.tile([P, T], F32, name="result")
+
+        def expert(e):
+            cols = slice(e * C, (e + 1) * C)
+            acc = bank_of(1, e)[:, 0, :]
+            for a in range(PASSES):
+                nc.tensor.matmul_mx(
+                    out=acc,
+                    lhsT=w_codes[:, e * PASSES + a, :].bitcast(FP8X4),
+                    lhsT_scale=w_scale[:, e * PASSES + a, :],
+                    rhs=x_codes[:, a, cols].bitcast(FP8X4),
+                    rhs_scale=x_scale[a][:, cols],
+                    start=(a == 0),
+                    stop=(a == PASSES - 1),
+                )
+
+        def add_bias(e):
+            nc.scalar.activation(y(e, 1), bank_of(1, e)[:, 0, :], IDENTITY, bias=bias[:, e : e + 1])
+
+        def scatter(first, count):
+            cols = slice(first * C, (first + count) * C)
+            nc.vector.tensor_tensor(result[:].indirect(slots(first * C, count * C)), y(first, count), gate_sb[:, cols], MULT)
+
+        round_wu(0, 0)
+        quantise_wu(0, 0)
+        quantise_u(1, early, u_stage(1, early))
+        round_wu(1, 0)
+        quantise_wu(1, 0)
+        round_wu(0, 1)
+        quantise_wu(0, 1)
+        for e in range(4):
+            project(0, e)
+        round_wu(1, 1)
+        quantise_wu(1, 1)
+        gather(1, 0, late, picked_late[:])
+        quantise_x(0, 0, 2)
+        gather(1, 1, late, picked_late[:])
+        quantise_x(0, 2, 2)
+        project(1, 0)
+        quantise_x(1, 0, 1)
+        expert(0)
+        add_bias(0)
+        interleave(late_stage[:], picked_late[:])
+        project(1, 1)
+        quantise_x(1, 1, 1)
+        expert(1)
+        add_bias(1)
+        quantise_u(1, late, late_stage[:])
+        for e in (2, 3):
+            project(1, e)
+            quantise_x(1, e, 1)
+            expert(e)
+        add_bias(2)
+        project(0, 4)
+        project(0, 5)
+        quantise_x(0, 4, 2)
+        for e in (4, 5):
+            project(1, e)
+            quantise_x(1, e, 1)
+            expert(e)
+        for e in (3, 4, 5):
+            add_bias(e)
+        for e in range(4):
+            scatter(e, 1)
+        scatter(4, 2)
+        nc.sync.dma_start(out=out, in_=result[:])

@@ -21,7 +21,7 @@ PASS = P * PACK
 PASSES = 2
 S = E * C
 PER_COLUMN = 16
-BANKS = ((0, 1, 2, 3, 0, 1), (4, 5, 6, 7, 2, 3))
+BANKS = ((0, 1, 2, 3, 4, 6), (4, 5, 6, 7, 5, 4))
 
 
 def tile_moe_prv_lin_bias_kernel(tc, uT, wu, w_words, w_scales, b, gate, offs, out):
@@ -59,12 +59,7 @@ def tile_moe_prv_lin_bias_kernel(tc, uT, wu, w_words, w_scales, b, gate, offs, o
                 nc.sync.dma_start(out=wu_raw[g, a][:], in_=wu_rows[g, a])
         w_codes = keep.tile([P, E * PASSES, N * PACK], U8, name="w_codes", align_bytes=64)
         w_src = w_words.rearrange("e a p n r -> p (e a) (n r)")
-
-        def load_w(half):
-            part = slice(half * E, (half + 1) * E)
-            nc.sync.dma_start(out=w_codes[:, part, :].bitcast(I32), in_=w_src[:, part, :].bitcast(I32))
-
-        load_w(0)
+        nc.sync.dma_start(out=w_codes[:].bitcast(I32), in_=w_src.bitcast(I32))
         w_scale = keep.tile([P, E * PASSES, N], U8, name="w_scale", align_bytes=64)
         nc.gpsimd.memset(w_scale[:].bitcast(I32), 0)
         scale_src = w_scales.rearrange("e a q n -> q (e a) n")
@@ -77,7 +72,6 @@ def tile_moe_prv_lin_bias_kernel(tc, uT, wu, w_words, w_scales, b, gate, offs, o
         nc.sync.dma_start(out=bias[:], in_=b)
         gate_sb = keep.tile([P, S], F32, name="gate_sb")
         nc.sync.dma_start(out=gate_sb[:], in_=gate)
-        load_w(1)
 
         u_codes = keep.tile([P, PASSES, S], U32, name="u_codes", align_bytes=64)
         u_scale = keep.tile([P, PASSES, S], U8, name="u_scale", align_bytes=64)
@@ -155,18 +149,23 @@ def tile_moe_prv_lin_bias_kernel(tc, uT, wu, w_words, w_scales, b, gate, offs, o
                 out=wu_codes[:, g, a, :].bitcast(FP8X4), scales=wu_scale[:, g, a, :], in_=wu_stage(g, a)
             )
 
-        x_grouped = keep.tile([P, PASSES, S * PACK], BF16, name="x_grouped", align_bytes=64)
+        x_grouped = keep.tile([P, PASSES * S * PACK], BF16, name="x_grouped", align_bytes=64)
         late_stage = keep.tile([P, 2 * C * PACK], BF16, name="late_stage", align_bytes=64)
-        x_codes = keep.tile([P, PASSES, S], U32, name="x_codes", align_bytes=64)
-        x_scale = [
-            shared.tile([P, S], U8, name="x_scale0", offset=0, align_bytes=64),
-            keep.tile([P, S], U8, name="x_scale1", align_bytes=64),
-        ]
+        x_codes = keep.tile([P, PASSES * S], U32, name="x_codes", align_bytes=64)
+        x_scale_first = shared.tile([P, 4 * C], U8, name="x_scale_first", offset=0, align_bytes=64)
+        x_scale_rest = keep.tile([P, PASSES * S], U8, name="x_scale_rest", align_bytes=64)
 
-        def x_stage(a, first, count):
-            if (a, first) == (1, 0):
+        def place(a, e):
+            return 4 * a + e if e < 4 else 2 * e + a
+
+        def x_scale(first, count):
+            tile = x_scale_first if first < 4 else x_scale_rest
+            return tile[:, first * C : (first + count) * C]
+
+        def x_stage(first, count):
+            if first == place(1, 2):
                 return late_stage[:, : C * PACK]
-            return x_grouped[:, a, first * C * PACK : (first + count) * C * PACK]
+            return x_grouped[:, first * C * PACK : (first + count) * C * PACK]
 
         def project(a, e):
             cols = slice(e * C, (e + 1) * C)
@@ -182,19 +181,21 @@ def tile_moe_prv_lin_bias_kernel(tc, uT, wu, w_words, w_scales, b, gate, offs, o
                         start=(g == 0),
                         stop=(g == PASSES - 1),
                     )
-            nc.scalar.copy(out=x_stage(a, e, 1).rearrange("p (s r) -> p s r", r=PACK), in_=bank[:].rearrange("p r s -> p s r"))
+            nc.scalar.copy(out=x_stage(place(a, e), 1).rearrange("p (s r) -> p s r", r=PACK), in_=bank[:].rearrange("p r s -> p s r"))
 
-        def quantise_x(a, first, count):
-            cols = slice(first * C, (first + count) * C)
+        def quantise_x(a, e, count):
+            first = place(a, e)
             nc.vector.quantize_mx(
-                out=x_codes[:, a, cols].bitcast(FP8X4), scales=x_scale[a][:, cols], in_=x_stage(a, first, count)
+                out=x_codes[:, first * C : (first + count) * C].bitcast(FP8X4),
+                scales=x_scale(first, count),
+                in_=x_stage(first, count),
             )
 
         y_own = keep.tile([P, S], F32, name="y_own")
 
         def y(first, count):
             if first == 3:
-                return x_stage(1, 4, 1).bitcast(F32)[:, :C]
+                return x_stage(place(0, 4), 1).bitcast(F32)[:, :C]
             return y_own[:, first * C : (first + count) * C]
 
         result = keep.tile([P, T], F32, name="result")
@@ -207,8 +208,8 @@ def tile_moe_prv_lin_bias_kernel(tc, uT, wu, w_words, w_scales, b, gate, offs, o
                     out=acc,
                     lhsT=w_codes[:, e * PASSES + a, :].bitcast(FP8X4),
                     lhsT_scale=w_scale[:, e * PASSES + a, :],
-                    rhs=x_codes[:, a, cols].bitcast(FP8X4),
-                    rhs_scale=x_scale[a][:, cols],
+                    rhs=x_codes[:, place(a, e) * C : (place(a, e) + 1) * C].bitcast(FP8X4),
+                    rhs_scale=x_scale(place(a, e), 1),
                     start=(a == 0),
                     stop=(a == PASSES - 1),
                 )
@@ -235,31 +236,24 @@ def tile_moe_prv_lin_bias_kernel(tc, uT, wu, w_words, w_scales, b, gate, offs, o
         quantise_x(0, 0, 2)
         gather(1, 1, late, picked_late[:])
         quantise_x(0, 2, 2)
-        project(1, 0)
-        quantise_x(1, 0, 1)
-        expert(0)
-        add_bias(0)
-        interleave(late_stage[:], picked_late[:])
-        project(1, 1)
-        quantise_x(1, 1, 1)
-        expert(1)
-        add_bias(1)
+        for e in range(4):
+            project(1, e)
+            quantise_x(1, e, 1)
+            if e == 2:
+                interleave(late_stage[:], picked_late[:])
         quantise_u(1, late, late_stage[:])
-        for e in (2, 3):
-            project(1, e)
-            quantise_x(1, e, 1)
+        for e in range(4):
             expert(e)
-        add_bias(2)
-        project(0, 4)
-        project(0, 5)
-        quantise_x(0, 4, 2)
+            if e < 3:
+                add_bias(e)
         for e in (4, 5):
+            project(0, e)
             project(1, e)
-            quantise_x(1, e, 1)
+            quantise_x(0, e, 2)
             expert(e)
         for e in (3, 4, 5):
             add_bias(e)
-        for e in range(4):
-            scatter(e, 1)
+        scatter(0, 3)
+        scatter(3, 1)
         scatter(4, 2)
         nc.sync.dma_start(out=out, in_=result[:])

@@ -130,7 +130,7 @@ def tile_moe_prv_lin_bias_kernel(tc, uT, wu, w_words, w_scales, b, gate, offs, o
 
         wu_codes = keep.tile([P, PASSES, PASSES, PASS], U32, name="wu_codes", align_bytes=64)
         wu_scale = keep.tile([P, PASSES, PASSES, PASS], U8, name="wu_scale", align_bytes=64)
-        vector_share = {(0, 0): 0, (1, 0): 0, (0, 1): 40, (1, 1): P}
+        vector_share = {(0, 0): 0, (1, 0): 0, (0, 1): 64, (1, 1): P}
 
         def wu_stage(g, a):
             return wu_grouped[:, min(2 * a + g, 2), :]
@@ -144,10 +144,15 @@ def tile_moe_prv_lin_bias_kernel(tc, uT, wu, w_words, w_scales, b, gate, offs, o
             if cut < P:
                 nc.scalar.copy(out=dst[:, cut:], in_=src[:, cut:])
 
-        def quantise_wu(g, a):
-            nc.vector.quantize_mx(
-                out=wu_codes[:, g, a, :].bitcast(FP8X4), scales=wu_scale[:, g, a, :], in_=wu_stage(g, a)
-            )
+        def quantise_wu(g, a, parts=1):
+            width = PASS // parts
+            for first in range(0, PASS, width):
+                words = slice(first, first + width)
+                nc.vector.quantize_mx(
+                    out=wu_codes[:, g, a, words].bitcast(FP8X4),
+                    scales=wu_scale[:, g, a, words],
+                    in_=wu_stage(g, a)[:, first * PACK : (first + width) * PACK],
+                )
 
         x_grouped = keep.tile([P, PASSES * S * PACK], BF16, name="x_grouped", align_bytes=64)
         late_stage = keep.tile([P, 2 * C * PACK], BF16, name="late_stage", align_bytes=64)
@@ -225,13 +230,17 @@ def tile_moe_prv_lin_bias_kernel(tc, uT, wu, w_words, w_scales, b, gate, offs, o
         quantise_wu(0, 0)
         quantise_u(1, early, u_stage(1, early))
         round_wu(1, 0)
-        quantise_wu(1, 0)
+        quantise_wu(1, 0, 2)
         round_wu(0, 1)
         quantise_wu(0, 1)
         for e in range(4):
             project(0, e)
-        round_wu(1, 1)
-        quantise_wu(1, 1)
+        last = wu_stage(1, 1)
+        dst = last.rearrange("p (r m j) -> p m j r", r=PACK, j=PACK)
+        src = wu_raw[1, 1][:].rearrange("p j (m r) -> p m j r", r=PACK)
+        for half in range(2):
+            nc.vector.tensor_copy(out=dst[:, :, :, 2 * half : 2 * half + 2], in_=src[:, :, :, 2 * half : 2 * half + 2])
+        quantise_wu(1, 1, 2)
         gather(1, 0, late, picked_late[:])
         quantise_x(0, 0, 2)
         gather(1, 1, late, picked_late[:])

@@ -14,6 +14,7 @@ U8 = mybir.dt.uint8
 FP8X4 = mybir.dt.float8_e4m3fn_x4
 IDENTITY = mybir.ActivationFunctionType.Identity
 MULT = mybir.AluOpType.mult
+ADD = mybir.AluOpType.add
 
 P = 128
 PACK = 4
@@ -21,7 +22,7 @@ PASS = P * PACK
 PASSES = 2
 S = E * C
 PER_COLUMN = 16
-BANKS = ((0, 1, 2, 3, 4, 6), (4, 5, 6, 7, 5, 4))
+WINDOW = 1024
 
 
 def tile_moe_prv_lin_bias_kernel(tc, uT, wu, w_words, w_scales, b, gate, offs, out):
@@ -33,132 +34,170 @@ def tile_moe_prv_lin_bias_kernel(tc, uT, wu, w_words, w_scales, b, gate, offs, o
         banks = [psum.tile([P, PACK, C], F32, name="bank%d" % i) for i in range(8)]
 
         def bank_of(a, e):
-            return banks[BANKS[a][e]]
+            return banks[((0, 1, 2, 3, 4, 4), (6, 7, 6, 7, 6, 7))[a][e]]
 
         offsets = keep.tile([P, S // PER_COLUMN], U16, name="offsets")
 
-        def slots(first, count):
-            return offsets[:, first // PER_COLUMN : (first + count) // PER_COLUMN]
+        def slots(cut):
+            return offsets[:, cut.start // PER_COLUMN : cut.stop // PER_COLUMN]
 
         u_rows = uT.rearrange("(g p h i) t -> g h p i t", g=PASSES, p=P, h=2)
+        halves = (slice(0, T // 2), slice(T // 2, T))
         u_raw = {}
         for g in range(PASSES):
             for h in range(2):
-                u_raw[g, h] = keep.tile([P, 2, T], F32, name="u_raw%d%d" % (g, h))
-                nc.sync.dma_start(out=u_raw[g, h][:], in_=u_rows[g, h])
-                if (g, h) == (0, 0):
-                    nc.sync.dma_start(offsets[:], offs)
+                for n, cut in enumerate(halves):
+                    if (g, h) == (1, 0):
+                        u_raw[g, h, n] = shared.tile([P, 2, T // 2], F32, name="u_raw10%d" % n, offset=16384 + 3072 * n, align_bytes=64)
+                    else:
+                        u_raw[g, h, n] = keep.tile([P, 2, T // 2], F32, name="u_raw%d%d%d" % (g, h, n))
+                    nc.sync.dma_start(out=u_raw[g, h, n][:], in_=u_rows[g, h][:, :, cut])
+                    if (g, h, n) == (0, 0, 1):
+                        nc.sync.dma_start(offsets[:], offs)
         wu_rows = wu.rearrange("(g p j) (a c) -> g a p j c", g=PASSES, p=P, a=PASSES)
         wu_raw = {}
-        for a in range(PASSES):
-            for g in range(PASSES):
-                if (g, a) == (1, 1):
-                    wu_raw[g, a] = shared.tile([P, PACK, PASS], F32, name="wu_raw11", offset=0, align_bytes=64)
-                else:
-                    wu_raw[g, a] = keep.tile([P, PACK, PASS], F32, name="wu_raw%d%d" % (g, a))
-                nc.sync.dma_start(out=wu_raw[g, a][:], in_=wu_rows[g, a])
-        w_codes = keep.tile([P, E * PASSES, N * PACK], U8, name="w_codes", align_bytes=64)
+        for g, a in ((0, 0), (1, 0), (0, 1)):
+            if a == 1:
+                w_scale = keep.tile([P, E * PASSES, N], U8, name="w_scale", align_bytes=64)
+                nc.gpsimd.memset(w_scale[:].bitcast(I32), 0)
+                scale_src = w_scales.rearrange("e a q n -> q (e a) n")
+                for quad in range(4):
+                    nc.sync.dma_start(
+                        out=w_scale[32 * quad : 32 * quad + 4, :, :].bitcast(I32),
+                        in_=scale_src[4 * quad : 4 * quad + 4].bitcast(I32),
+                    )
+                bias = keep.tile([P, E], F32, name="bias")
+                nc.sync.dma_start(out=bias[:], in_=b)
+                wu_raw[g, a] = shared.tile([P, PACK, PASS], F32, name="wu_raw01", offset=24576, align_bytes=64)
+            else:
+                wu_raw[g, a] = keep.tile([P, PACK, PASS], F32, name="wu_raw%d%d" % (g, a))
+            nc.sync.dma_start(out=wu_raw[g, a][:], in_=wu_rows[g, a])
+        last_raw = []
+        for n in range(2):
+            last_raw.append(shared.tile([P, PACK, PASS // 2], F32, name="last_raw%d" % n, offset=4096 + 4096 * n, align_bytes=64))
+            nc.sync.dma_start(out=last_raw[n][:], in_=wu_rows[1, 1][:, :, n * 256 : (n + 1) * 256])
         w_src = w_words.rearrange("e a p n r -> p (e a) (n r)")
-        nc.sync.dma_start(out=w_codes[:].bitcast(I32), in_=w_src.bitcast(I32))
-        w_scale = keep.tile([P, E * PASSES, N], U8, name="w_scale", align_bytes=64)
-        nc.gpsimd.memset(w_scale[:].bitcast(I32), 0)
-        scale_src = w_scales.rearrange("e a q n -> q (e a) n")
-        for quad in range(4):
-            nc.sync.dma_start(
-                out=w_scale[32 * quad : 32 * quad + 4, :, :].bitcast(I32),
-                in_=scale_src[4 * quad : 4 * quad + 4].bitcast(I32),
-            )
-        bias = keep.tile([P, E], F32, name="bias")
-        nc.sync.dma_start(out=bias[:], in_=b)
-        gate_sb = keep.tile([P, S], F32, name="gate_sb")
-        nc.sync.dma_start(out=gate_sb[:], in_=gate)
+        w_codes = {}
+        gates = {}
+        for first, count in ((0, 2), (2, 2), (4, 2)):
+            tile = keep.tile([P, count * PASSES, N * PACK], U8, name="w_codes%d" % first, align_bytes=64)
+            nc.sync.dma_start(out=tile[:].bitcast(I32), in_=w_src[:, first * PASSES : (first + count) * PASSES].bitcast(I32))
+            for e in range(first, first + count):
+                for a in range(PASSES):
+                    w_codes[e, a] = tile[:, (e - first) * PASSES + a, :]
+            gate_part = keep.tile([P, count * C], F32, name="gate%d" % first)
+            nc.sync.dma_start(out=gate_part[:], in_=gate[:, first * C : (first + count) * C])
+            for e in range(first, first + count):
+                gates[e] = gate_part[:, (e - first) * C : (e - first + 1) * C]
 
         u_codes = keep.tile([P, PASSES, S], U32, name="u_codes", align_bytes=64)
         u_scale = keep.tile([P, PASSES, S], U8, name="u_scale", align_bytes=64)
-        wu_grouped = keep.tile([P, 3, PASS * PACK], BF16, name="wu_grouped", align_bytes=64)
-        windows = {}
+        u_grouped = keep.tile([P, PASSES, S * PACK], BF16, name="u_grouped", align_bytes=64)
+        late_stage = shared.tile([P, 256 * PACK], BF16, name="late_stage", offset=8192, align_bytes=64)
 
-        def round_pairs(g, h):
-            pairs = keep.tile([P, T, 2], BF16, name="pairs%d%d" % (g, h))
-            src = u_raw[g, h][:].rearrange("p i t -> p t i")
+        first_grouped = shared.tile([P, S * PACK], BF16, name="first_grouped", offset=16384, align_bytes=64)
+
+        late_scale = keep.tile([P, 256], U8, name="late_scale", align_bytes=64)
+
+        early_scale = shared.tile([P, 512], U8, name="early_scale", offset=36864, align_bytes=64)
+
+        def u_plane(g, cut):
+            if g == 1 and cut.start < 512:
+                return early_scale[:, cut]
+            if g == 1 and cut.start >= 512:
+                return late_scale[:, cut.start - 512 : cut.stop - 512]
+            return u_scale[:, g, cut]
+
+        def u_stage(g, cut):
             if g == 0:
-                cut = (512, 256)[h]
-                nc.scalar.activation(pairs[:, cut:, :], src[:, cut:, :], IDENTITY)
-                nc.vector.tensor_copy(out=pairs[:, :cut, :], in_=src[:, :cut, :])
+                return first_grouped[:, cut.start * PACK : cut.stop * PACK]
+            if g == 1 and cut.start > 0:
+                return late_stage[:]
+            return u_grouped[:, g, cut.start * PACK : cut.stop * PACK]
+
+        pairs = {}
+        for g in range(PASSES):
+            for h in range(2):
+                if (g, h) == (1, 1):
+                    pairs[g, h] = shared.tile([P, T, 2], BF16, name="pairs11", offset=32768, align_bytes=64)
+                else:
+                    pairs[g, h] = keep.tile([P, WINDOW, 2], BF16, name="pairs%d%d" % (g, h))
+        for g, h in ((0, 0), (0, 1), (1, 0)):
+            nc.gpsimd.memset(pairs[g, h][:, T:, :].rearrange("p t i -> p (t i)").bitcast(U32), 0)
+
+        def round_pairs(g, h, n, cut, engine):
+            first = n * T // 2
+            dst = pairs[g, h][:, first + cut.start : first + cut.stop, :]
+            src = u_raw[g, h, n][:, :, cut].rearrange("p i t -> p t i")
+            if engine == "vector":
+                nc.vector.tensor_copy(out=dst, in_=src)
+            elif engine == "gpsimd":
+                nc.gpsimd.tensor_scalar(dst, src, 1.0, 0.0, MULT, ADD)
+            elif (g, h) == (0, 0):
+                nc.scalar.activation(dst, src, IDENTITY)
             else:
-                nc.scalar.copy(out=pairs[:], in_=src)
-            windows[g, h] = pairs[:].rearrange("p t i -> p (t i)").bitcast(U32)
+                nc.scalar.copy(out=dst, in_=src)
 
         def gather(g, h, cut, picked):
-            nc.vector.tensor_copy(out=picked[:, h, :], in_=windows[g, h].indirect(slots(cut.start, cut.stop - cut.start)))
+            window = pairs[g, h][:].rearrange("p t i -> p (t i)").bitcast(U32)
+            nc.vector.tensor_copy(out=picked, in_=window.indirect(slots(cut)))
 
-        u_grouped = keep.tile([P, PASSES, S * PACK], BF16, name="u_grouped", align_bytes=64)
-
-        def interleave(stage, picked):
+        def interleave(g, cut, picked):
+            stage = u_stage(g, cut)
             nc.vector.tensor_copy(
                 out=stage.rearrange("p (s h i) -> p s h i", h=2, i=2),
                 in_=picked.bitcast(BF16).rearrange("p h (s i) -> p s h i", i=2),
             )
 
-        def quantise_u(g, cut, stage):
+        def quantise_u(g, cut):
             nc.vector.quantize_mx(
                 out=u_codes[:, g, cut].bitcast(FP8X4),
-                scales=u_scale[:, g, cut],
-                in_=stage,
+                scales=u_plane(g, cut),
+                in_=u_stage(g, cut),
             )
 
-        early, late = slice(0, 512), slice(512, S)
-        picked0 = keep.tile([P, 2, S], U32, name="picked0")
-        for h in range(2):
-            round_pairs(0, h)
-            for cut in (early, late):
-                gather(0, h, cut, picked0[:, :, cut])
+        wu_codes = keep.tile([P, PASSES, PASSES * PASS], U32, name="wu_codes", align_bytes=64)
+        wu_scale = keep.tile([P, PASSES, PASSES * PASS], U8, name="wu_scale", align_bytes=64)
+        first_scale = shared.tile([P, PASS], U8, name="first_scale", offset=32768, align_bytes=64)
 
-        def u_stage(g, cut):
-            return u_grouped[:, g, cut.start * PACK : cut.stop * PACK]
+        def wu_plane(a, first, width):
+            if a == 0 and first < PASS:
+                return first_scale[:, first : first + width]
+            return wu_scale[:, a, first : first + width]
 
-        for cut in (early, late):
-            interleave(u_stage(0, cut), picked0[:, :, cut])
-        for cut in (early, late):
-            quantise_u(0, cut, u_stage(0, cut))
-        picked1 = keep.tile([P, 2, 512], U32, name="picked1")
-        picked_late = shared.tile([P, 2, 256], U32, name="picked_late", offset=1024, align_bytes=64)
-        for h in range(2):
-            round_pairs(1, h)
-            gather(1, h, early, picked1[:])
-        interleave(u_stage(1, early), picked1[:])
+        wu_stage = {}
+        for g in range(PASSES):
+            for a in range(PASSES):
+                if (g, a) == (0, 0):
+                    wu_stage[g, a] = shared.tile([P, PASS * PACK], BF16, name="wu_stage00", offset=36864, align_bytes=64)
+                else:
+                    wu_stage[g, a] = keep.tile([P, PASS * PACK], BF16, name="wu_stage%d%d" % (g, a), align_bytes=64)
 
-        wu_codes = keep.tile([P, PASSES, PASSES, PASS], U32, name="wu_codes", align_bytes=64)
-        wu_scale = keep.tile([P, PASSES, PASSES, PASS], U8, name="wu_scale", align_bytes=64)
-        vector_share = {(0, 0): 0, (1, 0): 0, (0, 1): 64, (1, 1): P}
+        def wu_place(g, a, r):
+            return (PACK * g + r) * P
 
-        def wu_stage(g, a):
-            return wu_grouped[:, min(2 * a + g, 2), :]
+        def round_wu(g, a, raw, first, cut, vector):
+            dst = wu_stage[g, a][:].rearrange("p (r m j) -> p m j r", r=PACK, j=PACK)[:, first + cut.start : first + cut.stop]
+            src = raw[:].rearrange("p j (m r) -> p m j r", r=PACK)[:, cut]
+            if vector:
+                nc.vector.tensor_copy(out=dst, in_=src)
+            else:
+                nc.scalar.copy(out=dst, in_=src)
 
-        def round_wu(g, a):
-            dst = wu_stage(g, a).rearrange("p (r m j) -> p m j r", r=PACK, j=PACK)
-            src = wu_raw[g, a][:].rearrange("p j (m r) -> p m j r", r=PACK)
-            cut = vector_share[g, a]
-            if cut > 0:
-                nc.vector.tensor_copy(out=dst[:, :cut], in_=src[:, :cut])
-            if cut < P:
-                nc.scalar.copy(out=dst[:, cut:], in_=src[:, cut:])
-
-        def quantise_wu(g, a, parts=1):
+        def quantise_wu(g, a, parts):
             width = PASS // parts
             for first in range(0, PASS, width):
-                words = slice(first, first + width)
+                words = slice(g * PASS + first, g * PASS + first + width)
                 nc.vector.quantize_mx(
-                    out=wu_codes[:, g, a, words].bitcast(FP8X4),
-                    scales=wu_scale[:, g, a, words],
-                    in_=wu_stage(g, a)[:, first * PACK : (first + width) * PACK],
+                    out=wu_codes[:, a, words].bitcast(FP8X4),
+                    scales=wu_plane(a, words.start, width),
+                    in_=wu_stage[g, a][:, first * PACK : (first + width) * PACK],
                 )
 
-        x_grouped = keep.tile([P, PASSES * S * PACK], BF16, name="x_grouped", align_bytes=64)
-        late_stage = keep.tile([P, 2 * C * PACK], BF16, name="late_stage", align_bytes=64)
         x_codes = keep.tile([P, PASSES * S], U32, name="x_codes", align_bytes=64)
-        x_scale_first = shared.tile([P, 4 * C], U8, name="x_scale_first", offset=0, align_bytes=64)
+        x_scale_first = shared.tile([P, 4 * C], U8, name="x_scale_first", offset=11264, align_bytes=64)
         x_scale_rest = keep.tile([P, PASSES * S], U8, name="x_scale_rest", align_bytes=64)
+        x_grouped = keep.tile([P, PASSES * S * PACK], BF16, name="x_grouped", align_bytes=64)
 
         def place(a, e):
             return 4 * a + e if e < 4 else 2 * e + a
@@ -167,26 +206,35 @@ def tile_moe_prv_lin_bias_kernel(tc, uT, wu, w_words, w_scales, b, gate, offs, o
             tile = x_scale_first if first < 4 else x_scale_rest
             return tile[:, first * C : (first + count) * C]
 
+        x_first = shared.tile([P, 4 * C * PACK], BF16, name="x_first", offset=24576, align_bytes=64)
+        x_stage10 = shared.tile([P, C * PACK], BF16, name="x_stage10", offset=12288, align_bytes=64)
+
         def x_stage(first, count):
-            if first == place(1, 2):
-                return late_stage[:, : C * PACK]
+            if first < 4:
+                return x_first[:, first * C * PACK : (first + count) * C * PACK]
+            if first == 4:
+                return x_stage10[:]
             return x_grouped[:, first * C * PACK : (first + count) * C * PACK]
 
-        def project(a, e):
+        def project(a, e, vector=False):
             cols = slice(e * C, (e + 1) * C)
             bank = bank_of(a, e)
             for r in range(PACK):
                 for g in range(PASSES):
                     nc.tensor.matmul_mx(
                         out=bank[:, r, :],
-                        lhsT=wu_codes[:, g, a, r * P : (r + 1) * P].bitcast(FP8X4),
-                        lhsT_scale=wu_scale[:, g, a, r * P : (r + 1) * P],
+                        lhsT=wu_codes[:, a, wu_place(g, a, r) : wu_place(g, a, r) + P].bitcast(FP8X4),
+                        lhsT_scale=wu_plane(a, wu_place(g, a, r), P),
                         rhs=u_codes[:, g, cols].bitcast(FP8X4),
-                        rhs_scale=u_scale[:, g, cols],
+                        rhs_scale=u_plane(g, cols),
                         start=(g == 0),
                         stop=(g == PASSES - 1),
                     )
-            nc.scalar.copy(out=x_stage(place(a, e), 1).rearrange("p (s r) -> p s r", r=PACK), in_=bank[:].rearrange("p r s -> p s r"))
+            dst = x_stage(place(a, e), 1).rearrange("p (s r) -> p s r", r=PACK)
+            if vector:
+                nc.vector.tensor_copy(out=dst, in_=bank[:].rearrange("p r s -> p s r"))
+            else:
+                nc.scalar.copy(out=dst, in_=bank[:].rearrange("p r s -> p s r"))
 
         def quantise_x(a, e, count):
             first = place(a, e)
@@ -196,73 +244,108 @@ def tile_moe_prv_lin_bias_kernel(tc, uT, wu, w_words, w_scales, b, gate, offs, o
                 in_=x_stage(first, count),
             )
 
-        y_own = keep.tile([P, S], F32, name="y_own")
-
-        def y(first, count):
-            if first == 3:
-                return x_stage(place(0, 4), 1).bitcast(F32)[:, :C]
-            return y_own[:, first * C : (first + count) * C]
-
+        y = keep.tile([P, S], F32, name="y")
         result = keep.tile([P, T], F32, name="result")
 
         def expert(e):
             cols = slice(e * C, (e + 1) * C)
-            acc = bank_of(1, e)[:, 0, :]
+            acc = banks[e % 4][:, 0, :]
             for a in range(PASSES):
+                words = slice(place(a, e) * C, (place(a, e) + 1) * C)
                 nc.tensor.matmul_mx(
                     out=acc,
-                    lhsT=w_codes[:, e * PASSES + a, :].bitcast(FP8X4),
+                    lhsT=w_codes[e, a].bitcast(FP8X4),
                     lhsT_scale=w_scale[:, e * PASSES + a, :],
-                    rhs=x_codes[:, place(a, e) * C : (place(a, e) + 1) * C].bitcast(FP8X4),
+                    rhs=x_codes[:, words].bitcast(FP8X4),
                     rhs_scale=x_scale(place(a, e), 1),
                     start=(a == 0),
                     stop=(a == PASSES - 1),
                 )
-
-        def add_bias(e):
-            nc.scalar.activation(y(e, 1), bank_of(1, e)[:, 0, :], IDENTITY, bias=bias[:, e : e + 1])
+            if e == 0:
+                nc.vector.tensor_scalar_add(y[:, cols], acc, bias[:, e : e + 1])
+            else:
+                nc.scalar.activation(y[:, cols], acc, IDENTITY, bias=bias[:, e : e + 1])
 
         def scatter(first, count):
             cols = slice(first * C, (first + count) * C)
-            nc.vector.tensor_tensor(result[:].indirect(slots(first * C, count * C)), y(first, count), gate_sb[:, cols], MULT)
+            nc.vector.tensor_tensor(result[:].indirect(slots(cols)), y[:, cols], gates[first], MULT)
 
-        round_wu(0, 0)
-        quantise_wu(0, 0)
-        quantise_u(1, early, u_stage(1, early))
-        round_wu(1, 0)
+        early, late = slice(0, 512), slice(512, S)
+        picked = [keep.tile([P, 2, S], U32, name="picked%d" % g) for g in range(PASSES)]
+        whole, half = slice(0, S), slice(0, T // 2)
+
+        round_pairs(0, 0, 0, half, "vector")
+        round_pairs(0, 0, 1, slice(0, 256), "vector")
+        round_pairs(0, 0, 1, slice(256, 384), "scalar")
+        gather(0, 0, whole, picked[0][:, 0, :])
+        round_pairs(0, 1, 0, half, "scalar")
+        round_pairs(0, 1, 1, half, "scalar")
+        gather(0, 1, whole, picked[0][:, 1, :])
+        round_pairs(1, 0, 0, half, "gpsimd")
+        round_pairs(1, 0, 1, half, "scalar")
+        gather(1, 0, whole, picked[1][:, 0, :])
+        nc.scalar.copy(
+            out=first_grouped[:].bitcast(U32).rearrange("p (s h) -> p s h", h=2),
+            in_=picked[0][:].rearrange("p h s -> p s h"),
+        )
+        for n in range(2):
+            round_pairs(1, 1, n, half, "gpsimd")
+        for cut in (early, late):
+            quantise_u(0, cut)
+        for cut in (early, late):
+            gather(1, 1, cut, picked[1][:, 1, cut])
+        interleave(1, early, picked[1][:, :, early])
+        round_wu(0, 0, wu_raw[0, 0], 0, slice(0, P), False)
+        quantise_wu(0, 0, 1)
+        quantise_u(1, early)
+        for n in range(2):
+            nc.tensor.matmul_mx(
+                out=banks[5][:].rearrange("p r s -> p (r s)"),
+                lhsT=wu_codes[:, 0, :P].bitcast(FP8X4),
+                lhsT_scale=wu_plane(0, 0, P),
+                rhs=u_codes[:, 0, early].bitcast(FP8X4),
+                rhs_scale=u_scale[:, 0, early],
+                start=True,
+                stop=True,
+            )
+        round_wu(1, 0, wu_raw[1, 0], 0, slice(0, P), False)
         quantise_wu(1, 0, 2)
-        round_wu(0, 1)
-        quantise_wu(0, 1)
+        round_wu(0, 1, wu_raw[0, 1], 0, slice(0, 44), True)
+        round_wu(0, 1, wu_raw[0, 1], 0, slice(44, P), False)
         for e in range(4):
             project(0, e)
-        last = wu_stage(1, 1)
-        dst = last.rearrange("p (r m j) -> p m j r", r=PACK, j=PACK)
-        src = wu_raw[1, 1][:].rearrange("p j (m r) -> p m j r", r=PACK)
-        for half in range(2):
-            nc.vector.tensor_copy(out=dst[:, :, :, 2 * half : 2 * half + 2], in_=src[:, :, :, 2 * half : 2 * half + 2])
+        round_wu(1, 1, last_raw[0], 0, slice(0, 64), True)
+        quantise_wu(0, 1, 1)
+        round_wu(1, 1, last_raw[1], 64, slice(0, 64), True)
         quantise_wu(1, 1, 2)
-        gather(1, 0, late, picked_late[:])
+        interleave(1, late, picked[1][:, :, late])
         quantise_x(0, 0, 2)
-        gather(1, 1, late, picked_late[:])
+        quantise_u(1, late)
+        project(1, 0)
+        quantise_x(1, 0, 1)
+        project(1, 1)
+        expert(0)
+        quantise_x(1, 1, 1)
         quantise_x(0, 2, 2)
-        for e in range(4):
-            project(1, e)
-            quantise_x(1, e, 1)
-            if e == 2:
-                interleave(late_stage[:], picked_late[:])
-        quantise_u(1, late, late_stage[:])
-        for e in range(4):
-            expert(e)
-            if e < 3:
-                add_bias(e)
-        for e in (4, 5):
-            project(0, e)
-            project(1, e)
-            quantise_x(0, e, 2)
-            expert(e)
-        for e in (3, 4, 5):
-            add_bias(e)
-        scatter(0, 3)
+        expert(1)
+        project(1, 2)
+        scatter(0, 1)
+        project(0, 4)
+        quantise_x(1, 2, 1)
+        expert(2)
+        project(1, 3)
+        scatter(1, 1)
+        quantise_x(1, 3, 1)
+        expert(3)
+        project(1, 4)
+        scatter(2, 1)
+        quantise_x(0, 4, 2)
+        expert(4)
+        project(0, 5)
+        project(1, 5)
         scatter(3, 1)
-        scatter(4, 2)
+        quantise_x(0, 5, 2)
+        expert(5)
+        for e in (4, 5):
+            scatter(e, 1)
         nc.sync.dma_start(out=out, in_=result[:])

@@ -42,18 +42,17 @@ def tile_moe_prv_lin_bias_kernel(tc, uT, wu, w_words, w_scales, b, gate, offs, o
             return offsets[:, cut.start // PER_COLUMN : cut.stop // PER_COLUMN]
 
         u_rows = uT.rearrange("(g p h i) t -> g h p i t", g=PASSES, p=P, h=2)
-        halves = (slice(0, T // 2), slice(T // 2, T))
         u_raw = {}
-        for g in range(PASSES):
-            for h in range(2):
-                for n, cut in enumerate(halves):
-                    if (g, h) == (1, 0):
-                        u_raw[g, h, n] = shared.tile([P, 2, T // 2], F32, name="u_raw10%d" % n, offset=16384 + 3072 * n, align_bytes=64)
-                    else:
-                        u_raw[g, h, n] = keep.tile([P, 2, T // 2], F32, name="u_raw%d%d%d" % (g, h, n))
-                    nc.sync.dma_start(out=u_raw[g, h, n][:], in_=u_rows[g, h][:, :, cut])
-                    if (g, h, n) == (0, 0, 1):
-                        nc.sync.dma_start(offsets[:], offs)
+        for n in range(2):
+            u_raw[0, 0, n] = keep.tile([P, 2, T // 2], F32, name="u_first%d" % n)
+            nc.sync.dma_start(out=u_raw[0, 0, n][:], in_=u_rows[0, 0][:, :, n * T // 2 : (n + 1) * T // 2])
+        nc.sync.dma_start(offsets[:], offs)
+        for g, h in ((0, 1), (1, 0), (1, 1)):
+            if (g, h) == (1, 0):
+                u_raw[g, h, 0] = shared.tile([P, 2, T], F32, name="u_raw10", offset=16384, align_bytes=64)
+            else:
+                u_raw[g, h, 0] = keep.tile([P, 2, T], F32, name="u_raw%d%d" % (g, h))
+            nc.sync.dma_start(out=u_raw[g, h, 0][:], in_=u_rows[g, h])
         wu_rows = wu.rearrange("(g p j) (a c) -> g a p j c", g=PASSES, p=P, a=PASSES)
         wu_raw = {}
         for g, a in ((0, 0), (1, 0), (0, 1)):
@@ -278,18 +277,18 @@ def tile_moe_prv_lin_bias_kernel(tc, uT, wu, w_words, w_scales, b, gate, offs, o
         round_pairs(0, 0, 1, slice(0, 256), "vector")
         round_pairs(0, 0, 1, slice(256, 384), "scalar")
         gather(0, 0, whole, picked[0][:, 0, :])
-        round_pairs(0, 1, 0, half, "scalar")
-        round_pairs(0, 1, 1, half, "scalar")
+        round_pairs(0, 1, 0, slice(0, 320), "gpsimd")
+        round_pairs(0, 1, 0, slice(320, T), "scalar")
         gather(0, 1, whole, picked[0][:, 1, :])
-        round_pairs(1, 0, 0, half, "gpsimd")
-        round_pairs(1, 0, 1, half, "scalar")
+        round_pairs(1, 0, 0, slice(0, 320), "gpsimd")
+        round_pairs(1, 0, 0, slice(320, T), "scalar")
         gather(1, 0, whole, picked[1][:, 0, :])
         nc.scalar.copy(
             out=first_grouped[:].bitcast(U32).rearrange("p (s h) -> p s h", h=2),
             in_=picked[0][:].rearrange("p h s -> p s h"),
         )
-        for n in range(2):
-            round_pairs(1, 1, n, half, "gpsimd")
+        round_pairs(1, 1, 0, slice(0, 448), "gpsimd")
+        round_pairs(1, 1, 0, slice(448, T), "scalar")
         for cut in (early, late):
             quantise_u(0, cut)
         for cut in (early, late):

@@ -297,16 +297,6 @@ def tile_moe_prv_lin_bias_kernel(tc, uT, wu, w_words, w_scales, b, gate, offs, o
         round_wu(0, 0, wu_raw[0, 0], 0, slice(0, P), False)
         quantise_wu(0, 0, 1)
         quantise_u(1, early)
-        for n in range(2):
-            nc.tensor.matmul_mx(
-                out=banks[5][:].rearrange("p r s -> p (r s)"),
-                lhsT=wu_codes[:, 0, :P].bitcast(FP8X4),
-                lhsT_scale=wu_plane(0, 0, P),
-                rhs=u_codes[:, 0, early].bitcast(FP8X4),
-                rhs_scale=u_scale[:, 0, early],
-                start=True,
-                stop=True,
-            )
         round_wu(1, 0, wu_raw[1, 0], 0, slice(0, P), False)
         quantise_wu(1, 0, 2)
         round_wu(0, 1, wu_raw[0, 1], 0, slice(0, 44), True)

@@ -71,23 +71,32 @@ def tile_moe_prv_lin_bias_kernel(tc, uT, wu, w_words, w_scales, b, gate, offs, o
             else:
                 wu_raw[g, a] = keep.tile([P, PACK, PASS], F32, name="wu_raw%d%d" % (g, a))
             nc.sync.dma_start(out=wu_raw[g, a][:], in_=wu_rows[g, a])
-        last_raw = []
-        for n in range(2):
-            last_raw.append(shared.tile([P, PACK, PASS // 2], F32, name="last_raw%d" % n, offset=4096 + 4096 * n, align_bytes=64))
-            nc.sync.dma_start(out=last_raw[n][:], in_=wu_rows[1, 1][:, :, n * 256 : (n + 1) * 256])
         w_src = w_words.rearrange("e a p n r -> p (e a) (n r)")
         w_codes = {}
         gates = {}
-        for first, count in ((0, 2), (2, 2), (4, 2)):
+
+        def load_words(first, count):
             tile = keep.tile([P, count * PASSES, N * PACK], U8, name="w_codes%d" % first, align_bytes=64)
             nc.sync.dma_start(out=tile[:].bitcast(I32), in_=w_src[:, first * PASSES : (first + count) * PASSES].bitcast(I32))
             for e in range(first, first + count):
                 for a in range(PASSES):
                     w_codes[e, a] = tile[:, (e - first) * PASSES + a, :]
-            gate_part = keep.tile([P, count * C], F32, name="gate%d" % first)
-            nc.sync.dma_start(out=gate_part[:], in_=gate[:, first * C : (first + count) * C])
+
+        def load_gate(first, count):
+            tile = keep.tile([P, count * C], F32, name="gate%d" % first)
+            nc.sync.dma_start(out=tile[:], in_=gate[:, first * C : (first + count) * C])
             for e in range(first, first + count):
-                gates[e] = gate_part[:, (e - first) * C : (e - first + 1) * C]
+                gates[e] = tile[:, (e - first) * C : (e - first + 1) * C]
+
+        last_raw = []
+        for n in range(2):
+            last_raw.append(shared.tile([P, PACK, PASS // 2], F32, name="last_raw%d" % n, offset=4096 + 4096 * n, align_bytes=64))
+            nc.sync.dma_start(out=last_raw[n][:], in_=wu_rows[1, 1][:, :, n * 256 : (n + 1) * 256])
+            load_words(n, 1)
+        load_gate(0, 2)
+        for first in (2, 4):
+            load_words(first, 2)
+            load_gate(first, 2)
 
         u_codes = keep.tile([P, PASSES, S], U32, name="u_codes", align_bytes=64)
         u_scale = keep.tile([P, PASSES, S], U8, name="u_scale", align_bytes=64)
@@ -305,7 +314,10 @@ def tile_moe_prv_lin_bias_kernel(tc, uT, wu, w_words, w_scales, b, gate, offs, o
             project(0, e)
         round_wu(1, 1, last_raw[0], 0, slice(0, 64), True)
         quantise_wu(0, 1, 1)
-        round_wu(1, 1, last_raw[1], 64, slice(0, 64), True)
+        dst = wu_stage[1, 1][:].rearrange("p (r m j) -> p m j r", r=PACK, j=PACK)[:, 64:]
+        src = last_raw[1][:].rearrange("p j (m r) -> p m j r", r=PACK)
+        for pair in (slice(0, 2), slice(2, 4)):
+            nc.vector.tensor_copy(out=dst[:, :, :, pair], in_=src[:, :, :, pair])
         quantise_wu(1, 1, 2)
         interleave(1, late, picked[1][:, :, late])
         quantise_x(0, 0, 2)

@@ -23,6 +23,13 @@ PASSES = 2
 S = E * C
 PER_COLUMN = 16
 WINDOW = 1024
+DEPTH = 3
+STAGE = 2 * PASS * 2
+RING = 8 * STAGE
+EVERY = slice(0, 4)
+PLACE = {(0, 0, 0): 10, (1, 0, 0): 24, (0, 1, 0): 28, (0, 1, 2): 26, (1, 1, 0): 0, (1, 1, 2): 2}
+EARLY, LATE = slice(0, 512), slice(512, S)
+PAIRS = (slice(0, 2), slice(2, 4))
 
 
 def tile_moe_prv_lin_bias_kernel(tc, uT, wu, w_words, w_scales, b, gate, offs, out):
@@ -34,7 +41,10 @@ def tile_moe_prv_lin_bias_kernel(tc, uT, wu, w_words, w_scales, b, gate, offs, o
         banks = [psum.tile([P, PACK, C], F32, name="bank%d" % i) for i in range(8)]
 
         def bank_of(a, e):
-            return banks[((0, 1, 2, 3, 4, 4), (6, 7, 6, 7, 6, 7))[a][e]]
+            return banks[((0, 1, 2, 3, 4, 2), (5, 6, 7, 0, 1, 3))[a][e]]
+
+        def sum_bank(e):
+            return banks[e + 2]
 
         offsets = keep.tile([P, S // PER_COLUMN], U16, name="offsets")
 
@@ -48,32 +58,24 @@ def tile_moe_prv_lin_bias_kernel(tc, uT, wu, w_words, w_scales, b, gate, offs, o
             nc.sync.dma_start(out=u_raw[0, 0, n][:], in_=u_rows[0, 0][:, :, n * T // 2 : (n + 1) * T // 2])
         nc.sync.dma_start(offsets[:], offs)
         for g, h in ((0, 1), (1, 0), (1, 1)):
-            if (g, h) == (1, 0):
-                u_raw[g, h, 0] = shared.tile([P, 2, T], F32, name="u_raw10", offset=16384, align_bytes=64)
-            else:
-                u_raw[g, h, 0] = keep.tile([P, 2, T], F32, name="u_raw%d%d" % (g, h))
+            u_raw[g, h, 0] = keep.tile([P, 2, T], F32, name="u_raw%d%d" % (g, h))
             nc.sync.dma_start(out=u_raw[g, h, 0][:], in_=u_rows[g, h])
         wu_rows = wu.rearrange("(g p j) (a c) -> g a p j c", g=PASSES, p=P, a=PASSES)
         wu_raw = {}
         for g, a in ((0, 0), (1, 0), (0, 1)):
             if a == 1:
-                w_scale = keep.tile([P, E * PASSES, N], U8, name="w_scale", align_bytes=64)
-                nc.gpsimd.memset(w_scale[:].bitcast(I32), 0)
-                scale_src = w_scales.rearrange("e a q n -> q (e a) n")
-                for quad in range(4):
-                    nc.sync.dma_start(
-                        out=w_scale[32 * quad : 32 * quad + 4, :, :].bitcast(I32),
-                        in_=scale_src[4 * quad : 4 * quad + 4].bitcast(I32),
-                    )
-                bias = keep.tile([P, E], F32, name="bias")
-                nc.sync.dma_start(out=bias[:], in_=b)
-                wu_raw[g, a] = shared.tile([P, PACK, PASS], F32, name="wu_raw01", offset=24576, align_bytes=64)
+                wu_raw[g, a] = shared.tile([P, PACK, PASS], F32, name="wu_raw%d%d" % (g, a), offset=0, align_bytes=64)
             else:
                 wu_raw[g, a] = keep.tile([P, PACK, PASS], F32, name="wu_raw%d%d" % (g, a))
             nc.sync.dma_start(out=wu_raw[g, a][:], in_=wu_rows[g, a])
+        last_raw = []
+        for n in range(2):
+            last_raw.append(keep.tile([P, PACK, PASS // 2], F32, name="last_raw%d" % n))
+            nc.sync.dma_start(out=last_raw[n][:], in_=wu_rows[1, 1][:, :, n * 256 : (n + 1) * 256])
+
         w_src = w_words.rearrange("e a p n r -> p (e a) (n r)")
         w_codes = {}
-        gates = {}
+        gate_tiles = {}
 
         def load_words(first, count):
             tile = keep.tile([P, count * PASSES, N * PACK], U8, name="w_codes%d" % first, align_bytes=64)
@@ -85,53 +87,63 @@ def tile_moe_prv_lin_bias_kernel(tc, uT, wu, w_words, w_scales, b, gate, offs, o
         def load_gate(first, count):
             tile = keep.tile([P, count * C], F32, name="gate%d" % first)
             nc.sync.dma_start(out=tile[:], in_=gate[:, first * C : (first + count) * C])
-            for e in range(first, first + count):
-                gates[e] = tile[:, (e - first) * C : (e - first + 1) * C]
+            gate_tiles[first * C] = tile
 
-        last_raw = []
-        for n in range(2):
-            last_raw.append(shared.tile([P, PACK, PASS // 2], F32, name="last_raw%d" % n, offset=4096 + 4096 * n, align_bytes=64))
-            nc.sync.dma_start(out=last_raw[n][:], in_=wu_rows[1, 1][:, :, n * 256 : (n + 1) * 256])
-            load_words(n, 1)
-        load_gate(0, 2)
-        for first in (2, 4):
-            load_words(first, 2)
-            load_gate(first, 2)
+        def gates(cut):
+            first = max(start for start in gate_tiles if start <= cut.start)
+            return gate_tiles[first][:, cut.start - first : cut.stop - first]
 
-        u_codes = keep.tile([P, PASSES, S], U32, name="u_codes", align_bytes=64)
-        u_scale = keep.tile([P, PASSES, S], U8, name="u_scale", align_bytes=64)
-        u_grouped = keep.tile([P, PASSES, S * PACK], BF16, name="u_grouped", align_bytes=64)
-        late_stage = shared.tile([P, 256 * PACK], BF16, name="late_stage", offset=8192, align_bytes=64)
+        w_scale = keep.tile([P, E * PASSES, N], U8, name="w_scale", align_bytes=64)
+        nc.gpsimd.memset(w_scale[:].bitcast(I32), 0)
+        scale_src = w_scales.rearrange("e a q n -> q (e a) n")
+        for quad in range(4):
+            nc.sync.dma_start(
+                out=w_scale[32 * quad : 32 * quad + 4, :, :].bitcast(I32),
+                in_=scale_src[4 * quad : 4 * quad + 4].bitcast(I32),
+            )
+        bias = keep.tile([P, E], F32, name="bias")
+        nc.sync.dma_start(out=bias[:], in_=b)
+        load_gate(0, DEPTH)
+        load_words(0, E)
+        load_gate(DEPTH, E - DEPTH)
 
-        first_grouped = shared.tile([P, S * PACK], BF16, name="first_grouped", offset=16384, align_bytes=64)
+        def parts(g, a):
+            return (EVERY,) if a == 0 else PAIRS
 
-        late_scale = keep.tile([P, 256], U8, name="late_scale", align_bytes=64)
+        wu_codes, wu_scale, wu_stage = {}, {}, {}
+        for a in range(PASSES):
+            for g in range(PASSES):
+                for rs in parts(g, a):
+                    n, count = rs.start, rs.stop - rs.start
+                    if (g, a, n) == (1, 1, 2):
+                        wu_codes[g, a, n] = shared.tile([P, count * P], U32, name="wu_codes_last", offset=RING + STAGE, align_bytes=64)
+                    else:
+                        wu_codes[g, a, n] = keep.tile([P, count * P], U32, name="wu_codes%d%d%d" % (g, a, n), align_bytes=64)
+                    wu_scale[g, a, n] = keep.tile([P, count * P], U8, name="wu_scale%d%d%d" % (g, a, n), align_bytes=64)
+                    wu_stage[g, a, n] = shared.tile(
+                        [P, count * PASS], BF16, name="wu_stage%d%d%d" % (g, a, n), offset=PLACE[g, a, n] * STAGE // 2, align_bytes=64
+                    )
 
-        early_scale = shared.tile([P, 512], U8, name="early_scale", offset=36864, align_bytes=64)
+        u_codes = [keep.tile([P, S], U32, name="u_codes%d" % g, align_bytes=64) for g in range(PASSES)]
+        u_scale = [keep.tile([P, S], U8, name="u_scale%d" % g, align_bytes=64) for g in range(PASSES)]
+        late_scale = shared.tile([P, S - LATE.start], U8, name="late_scale", offset=12 * STAGE, align_bytes=64)
 
         def u_plane(g, cut):
-            if g == 1 and cut.start < 512:
-                return early_scale[:, cut]
-            if g == 1 and cut.start >= 512:
-                return late_scale[:, cut.start - 512 : cut.stop - 512]
-            return u_scale[:, g, cut]
+            if g == 1 and cut.start >= LATE.start:
+                return late_scale[:, cut.start - LATE.start : cut.stop - LATE.start]
+            return u_scale[g][:, cut]
 
-        def u_stage(g, cut):
-            if g == 0:
-                return first_grouped[:, cut.start * PACK : cut.stop * PACK]
-            if g == 1 and cut.start > 0:
-                return late_stage[:]
-            return u_grouped[:, g, cut.start * PACK : cut.stop * PACK]
+        u_stage = [
+            keep.tile([P, S * PACK], BF16, name="u_stage0", align_bytes=64),
+            shared.tile([P, S * PACK], BF16, name="u_stage1", offset=5 * STAGE, align_bytes=64),
+        ]
 
         pairs = {}
         for g in range(PASSES):
             for h in range(2):
-                if (g, h) == (1, 1):
-                    pairs[g, h] = shared.tile([P, T, 2], BF16, name="pairs11", offset=32768, align_bytes=64)
-                else:
-                    pairs[g, h] = keep.tile([P, WINDOW, 2], BF16, name="pairs%d%d" % (g, h))
-        for g, h in ((0, 0), (0, 1), (1, 0)):
-            nc.gpsimd.memset(pairs[g, h][:, T:, :].rearrange("p t i -> p (t i)").bitcast(U32), 0)
+                pairs[g, h] = keep.tile([P, WINDOW, 2], BF16, name="pairs%d%d" % (g, h))
+                nc.gpsimd.memset(pairs[g, h][:, T:, :].rearrange("p t i -> p (t i)").bitcast(U32), 0)
+        picked = [keep.tile([P, 2, S], U32, name="picked%d" % g) for g in range(PASSES)]
 
         def round_pairs(g, h, n, cut, engine):
             first = n * T // 2
@@ -146,207 +158,188 @@ def tile_moe_prv_lin_bias_kernel(tc, uT, wu, w_words, w_scales, b, gate, offs, o
             else:
                 nc.scalar.copy(out=dst, in_=src)
 
-        def gather(g, h, cut, picked):
+        def gather(g, h):
             window = pairs[g, h][:].rearrange("p t i -> p (t i)").bitcast(U32)
-            nc.vector.tensor_copy(out=picked, in_=window.indirect(slots(cut)))
-
-        def interleave(g, cut, picked):
-            stage = u_stage(g, cut)
-            nc.vector.tensor_copy(
-                out=stage.rearrange("p (s h i) -> p s h i", h=2, i=2),
-                in_=picked.bitcast(BF16).rearrange("p h (s i) -> p s h i", i=2),
-            )
+            nc.vector.tensor_copy(out=picked[g][:, h, :], in_=window.indirect(offsets[:]))
 
         def quantise_u(g, cut):
             nc.vector.quantize_mx(
-                out=u_codes[:, g, cut].bitcast(FP8X4),
+                out=u_codes[g][:, cut].bitcast(FP8X4),
                 scales=u_plane(g, cut),
-                in_=u_stage(g, cut),
+                in_=u_stage[g][:, cut.start * PACK : cut.stop * PACK],
             )
 
-        wu_codes = keep.tile([P, PASSES, PASSES * PASS], U32, name="wu_codes", align_bytes=64)
-        wu_scale = keep.tile([P, PASSES, PASSES * PASS], U8, name="wu_scale", align_bytes=64)
-        first_scale = shared.tile([P, PASS], U8, name="first_scale", offset=32768, align_bytes=64)
-
-        def wu_plane(a, first, width):
-            if a == 0 and first < PASS:
-                return first_scale[:, first : first + width]
-            return wu_scale[:, a, first : first + width]
-
-        wu_stage = {}
-        for g in range(PASSES):
-            for a in range(PASSES):
-                if (g, a) == (0, 0):
-                    wu_stage[g, a] = shared.tile([P, PASS * PACK], BF16, name="wu_stage00", offset=36864, align_bytes=64)
-                else:
-                    wu_stage[g, a] = keep.tile([P, PASS * PACK], BF16, name="wu_stage%d%d" % (g, a), align_bytes=64)
-
-        def wu_place(g, a, r):
-            return (PACK * g + r) * P
-
-        def round_wu(g, a, raw, first, cut, vector):
-            dst = wu_stage[g, a][:].rearrange("p (r m j) -> p m j r", r=PACK, j=PACK)[:, first + cut.start : first + cut.stop]
-            src = raw[:].rearrange("p j (m r) -> p m j r", r=PACK)[:, cut]
-            if vector:
+        def round_wu(g, a, raw, first, cut, pair, engine):
+            dst = wu_stage[g, a, pair.start][:].rearrange("p (r m j) -> p m j r", m=P, j=PACK)[:, first + cut.start : first + cut.stop]
+            src = raw[:].rearrange("p j (m r) -> p m j r", r=PACK)[:, cut, :, pair]
+            if engine == "vector":
                 nc.vector.tensor_copy(out=dst, in_=src)
+            elif engine == "gpsimd":
+                walk = "p m j r -> p m r j"
+                nc.gpsimd.tensor_scalar(dst.rearrange(walk), src.rearrange(walk), 1.0, 0.0, MULT, ADD)
             else:
                 nc.scalar.copy(out=dst, in_=src)
 
-        def quantise_wu(g, a, parts):
-            width = PASS // parts
-            for first in range(0, PASS, width):
-                words = slice(g * PASS + first, g * PASS + first + width)
-                nc.vector.quantize_mx(
-                    out=wu_codes[:, a, words].bitcast(FP8X4),
-                    scales=wu_plane(a, words.start, width),
-                    in_=wu_stage[g, a][:, first * PACK : (first + width) * PACK],
-                )
-
-        x_codes = keep.tile([P, PASSES * S], U32, name="x_codes", align_bytes=64)
-        x_scale_first = shared.tile([P, 4 * C], U8, name="x_scale_first", offset=11264, align_bytes=64)
-        x_scale_rest = keep.tile([P, PASSES * S], U8, name="x_scale_rest", align_bytes=64)
-        x_grouped = keep.tile([P, PASSES * S * PACK], BF16, name="x_grouped", align_bytes=64)
-
-        def place(a, e):
-            return 4 * a + e if e < 4 else 2 * e + a
-
-        def x_scale(first, count):
-            tile = x_scale_first if first < 4 else x_scale_rest
-            return tile[:, first * C : (first + count) * C]
-
-        x_first = shared.tile([P, 4 * C * PACK], BF16, name="x_first", offset=24576, align_bytes=64)
-        x_stage10 = shared.tile([P, C * PACK], BF16, name="x_stage10", offset=12288, align_bytes=64)
-
-        def x_stage(first, count):
-            if first < 4:
-                return x_first[:, first * C * PACK : (first + count) * C * PACK]
-            if first == 4:
-                return x_stage10[:]
-            return x_grouped[:, first * C * PACK : (first + count) * C * PACK]
-
-        def project(a, e, vector=False):
-            cols = slice(e * C, (e + 1) * C)
-            bank = bank_of(a, e)
-            for r in range(PACK):
-                for g in range(PASSES):
-                    nc.tensor.matmul_mx(
-                        out=bank[:, r, :],
-                        lhsT=wu_codes[:, a, wu_place(g, a, r) : wu_place(g, a, r) + P].bitcast(FP8X4),
-                        lhsT_scale=wu_plane(a, wu_place(g, a, r), P),
-                        rhs=u_codes[:, g, cols].bitcast(FP8X4),
-                        rhs_scale=u_plane(g, cols),
-                        start=(g == 0),
-                        stop=(g == PASSES - 1),
-                    )
-            dst = x_stage(place(a, e), 1).rearrange("p (s r) -> p s r", r=PACK)
-            if vector:
-                nc.vector.tensor_copy(out=dst, in_=bank[:].rearrange("p r s -> p s r"))
-            else:
-                nc.scalar.copy(out=dst, in_=bank[:].rearrange("p r s -> p s r"))
-
-        def quantise_x(a, e, count):
-            first = place(a, e)
+        def quantise_wu(g, a, rs):
             nc.vector.quantize_mx(
-                out=x_codes[:, first * C : (first + count) * C].bitcast(FP8X4),
-                scales=x_scale(first, count),
-                in_=x_stage(first, count),
+                out=wu_codes[g, a, rs.start][:].bitcast(FP8X4),
+                scales=wu_scale[g, a, rs.start][:],
+                in_=wu_stage[g, a, rs.start][:],
             )
 
+        x_stage, x_codes, x_scale = {}, {}, {}
+        groups = [[(0, e) for e in range(4)]] + [[(0, 4)]] + [[(1, e)] for e in range(5)] + [[(0, 5), (1, 5)]]
+        group_tiles = {}
+        for n, group in enumerate(groups):
+            width = len(group) * C
+            if group in ([(1, DEPTH)], [(1, DEPTH + 1)]):
+                stage = shared.tile([P, width * PACK], BF16, name="x_stage%d" % n, offset=RING + 1024 * (group[0][1] - DEPTH), align_bytes=64)
+            else:
+                stage = keep.tile([P, width * PACK], BF16, name="x_stage%d" % n, align_bytes=64)
+            if group in ([(1, 0)], [(1, 1)]):
+                codes = shared.tile([P, width], U32, name="x_codes%d" % n, offset=RING + 1024 * group[0][1], align_bytes=64)
+            else:
+                codes = keep.tile([P, width], U32, name="x_codes%d" % n, align_bytes=64)
+            if n < 2:
+                scale = shared.tile([P, width], U8, name="x_scale%d" % n, offset=512 * n, align_bytes=64)
+            else:
+                scale = keep.tile([P, width], U8, name="x_scale%d" % n, align_bytes=64)
+            group_tiles[group[-1]] = (stage, codes, scale)
+            for i, key in enumerate(group):
+                x_stage[key] = stage[:, i * C * PACK : (i + 1) * C * PACK]
+                x_codes[key] = codes[:, i * C : (i + 1) * C]
+                x_scale[key] = scale[:, i * C : (i + 1) * C]
+
+        def columns(e):
+            return slice(e * C, (e + 1) * C)
+
+        def project(a, e, g):
+            order = (2, 3, 0, 1) if (g, a) == (0, 1) else (0, 1, 2, 3)
+            for r in order:
+                first = max(rs.start for rs in parts(g, a) if rs.start <= r)
+                words = slice((r - first) * P, (r - first + 1) * P)
+                nc.tensor.matmul_mx(
+                    out=bank_of(a, e)[:, r, :],
+                    lhsT=wu_codes[g, a, first][:, words].bitcast(FP8X4),
+                    lhsT_scale=wu_scale[g, a, first][:, words],
+                    rhs=u_codes[g][:, columns(e)].bitcast(FP8X4),
+                    rhs_scale=u_plane(g, columns(e)),
+                    start=(g == 0 and r == order[0]),
+                    stop=(g == PASSES - 1 and r == PACK - 1),
+                )
+
+        def empty(a, e):
+            nc.scalar.copy(
+                out=x_stage[a, e].rearrange("p (s r) -> p s r", r=PACK),
+                in_=bank_of(a, e)[:].rearrange("p r s -> p s r"),
+            )
+
+        def quantise_x(a, e):
+            stage, codes, scale = group_tiles[a, e]
+            nc.vector.quantize_mx(out=codes[:].bitcast(FP8X4), scales=scale[:], in_=stage[:])
+
         y = keep.tile([P, S], F32, name="y")
+        y_late = shared.tile([P, 2 * C], F32, name="y_late", offset=RING + STAGE, align_bytes=64)
+
+        def sums(cut):
+            if cut.start in (3 * C, 4 * C):
+                return y_late[:, cut.start - 3 * C : cut.stop - 3 * C]
+            return y[:, cut]
+
         result = keep.tile([P, T], F32, name="result")
 
         def expert(e):
-            cols = slice(e * C, (e + 1) * C)
-            acc = banks[e % 4][:, 0, :]
+            acc = sum_bank(e)[:, 0, :]
             for a in range(PASSES):
-                words = slice(place(a, e) * C, (place(a, e) + 1) * C)
                 nc.tensor.matmul_mx(
                     out=acc,
                     lhsT=w_codes[e, a].bitcast(FP8X4),
                     lhsT_scale=w_scale[:, e * PASSES + a, :],
-                    rhs=x_codes[:, words].bitcast(FP8X4),
-                    rhs_scale=x_scale(place(a, e), 1),
+                    rhs=x_codes[a, e].bitcast(FP8X4),
+                    rhs_scale=x_scale[a, e],
                     start=(a == 0),
                     stop=(a == PASSES - 1),
                 )
-            if e == 0:
-                nc.vector.tensor_scalar_add(y[:, cols], acc, bias[:, e : e + 1])
-            else:
-                nc.scalar.activation(y[:, cols], acc, IDENTITY, bias=bias[:, e : e + 1])
+
+        def add_bias(e):
+            nc.scalar.activation(sums(columns(e)), sum_bank(e)[:, 0, :], IDENTITY, bias=bias[:, e : e + 1])
 
         def scatter(first, count):
-            cols = slice(first * C, (first + count) * C)
-            nc.vector.tensor_tensor(result[:].indirect(slots(cols)), y[:, cols], gates[first], MULT)
+            cut = slice(first * C, (first + count) * C)
+            nc.vector.tensor_tensor(result[:].indirect(slots(cut)), sums(cut), gates(cut), MULT)
 
-        early, late = slice(0, 512), slice(512, S)
-        picked = [keep.tile([P, 2, S], U32, name="picked%d" % g) for g in range(PASSES)]
-        whole, half = slice(0, S), slice(0, T // 2)
+        half, whole = slice(0, T // 2), slice(0, P)
 
         round_pairs(0, 0, 0, half, "vector")
         round_pairs(0, 0, 1, slice(0, 256), "vector")
         round_pairs(0, 0, 1, slice(256, 384), "scalar")
-        gather(0, 0, whole, picked[0][:, 0, :])
+        gather(0, 0)
         round_pairs(0, 1, 0, slice(0, 320), "gpsimd")
         round_pairs(0, 1, 0, slice(320, T), "scalar")
-        gather(0, 1, whole, picked[0][:, 1, :])
+        gather(0, 1)
         round_pairs(1, 0, 0, slice(0, 320), "gpsimd")
         round_pairs(1, 0, 0, slice(320, T), "scalar")
-        gather(1, 0, whole, picked[1][:, 0, :])
+        gather(1, 0)
         nc.scalar.copy(
-            out=first_grouped[:].bitcast(U32).rearrange("p (s h) -> p s h", h=2),
+            out=u_stage[0][:].bitcast(U32).rearrange("p (s h) -> p s h", h=2),
             in_=picked[0][:].rearrange("p h s -> p s h"),
         )
         round_pairs(1, 1, 0, slice(0, 448), "gpsimd")
         round_pairs(1, 1, 0, slice(448, T), "scalar")
-        for cut in (early, late):
+        for cut in (EARLY, LATE):
             quantise_u(0, cut)
-        for cut in (early, late):
-            gather(1, 1, cut, picked[1][:, 1, cut])
-        interleave(1, early, picked[1][:, :, early])
-        round_wu(0, 0, wu_raw[0, 0], 0, slice(0, P), False)
-        quantise_wu(0, 0, 1)
-        quantise_u(1, early)
-        round_wu(1, 0, wu_raw[1, 0], 0, slice(0, P), False)
-        quantise_wu(1, 0, 2)
-        round_wu(0, 1, wu_raw[0, 1], 0, slice(0, 44), True)
-        round_wu(0, 1, wu_raw[0, 1], 0, slice(44, P), False)
-        for e in range(4):
-            project(0, e)
-        round_wu(1, 1, last_raw[0], 0, slice(0, 64), True)
-        quantise_wu(0, 1, 1)
-        dst = wu_stage[1, 1][:].rearrange("p (r m j) -> p m j r", r=PACK, j=PACK)[:, 64:]
-        src = last_raw[1][:].rearrange("p j (m r) -> p m j r", r=PACK)
-        for pair in (slice(0, 2), slice(2, 4)):
-            nc.vector.tensor_copy(out=dst[:, :, :, pair], in_=src[:, :, :, pair])
-        quantise_wu(1, 1, 2)
-        interleave(1, late, picked[1][:, :, late])
-        quantise_x(0, 0, 2)
-        quantise_u(1, late)
-        project(1, 0)
-        quantise_x(1, 0, 1)
-        project(1, 1)
-        expert(0)
-        quantise_x(1, 1, 1)
-        quantise_x(0, 2, 2)
-        expert(1)
-        project(1, 2)
-        scatter(0, 1)
-        project(0, 4)
-        quantise_x(1, 2, 1)
-        expert(2)
-        project(1, 3)
-        scatter(1, 1)
-        quantise_x(1, 3, 1)
-        expert(3)
-        project(1, 4)
-        scatter(2, 1)
-        quantise_x(0, 4, 2)
-        expert(4)
-        project(0, 5)
-        project(1, 5)
-        scatter(3, 1)
-        quantise_x(0, 5, 2)
-        expert(5)
-        for e in (4, 5):
+        gather(1, 1)
+        round_wu(0, 0, wu_raw[0, 0], 0, slice(0, 48), EVERY, "gpsimd")
+        round_wu(0, 0, wu_raw[0, 0], 0, slice(48, P), EVERY, "scalar")
+        quantise_wu(0, 0, EVERY)
+        for cut in (EARLY, LATE):
+            nc.vector.tensor_copy(
+                out=u_stage[1][:].rearrange("p (s h i) -> p s h i", h=2, i=2)[:, cut],
+                in_=picked[1][:].bitcast(BF16).rearrange("p h (s i) -> p s h i", i=2)[:, cut],
+            )
+        round_wu(1, 0, wu_raw[1, 0], 0, slice(0, 24), EVERY, "vector")
+        round_wu(1, 0, wu_raw[1, 0], 0, slice(24, P), EVERY, "scalar")
+        quantise_u(1, EARLY)
+        for e in range(E - 1):
+            project(0, e, 0)
+        quantise_wu(1, 0, EVERY)
+        round_wu(0, 1, wu_raw[0, 1], 0, whole, PAIRS[0], "scalar")
+        round_wu(0, 1, wu_raw[0, 1], 0, whole, PAIRS[1], "vector")
+        quantise_u(1, LATE)
+        for e in range(E - 1):
+            project(0, e, 1)
+            empty(0, e)
+        for pair in reversed(PAIRS):
+            quantise_wu(0, 1, pair)
+        for e in range(E - 1):
+            project(1, e, 0)
+        for n in range(2):
+            for pair in PAIRS:
+                round_wu(1, 1, last_raw[n], 64 * n, slice(0, 64), pair, "vector")
+        for pair in PAIRS:
+            quantise_wu(1, 1, pair)
+        quantise_x(0, 3)
+        quantise_x(0, 4)
+        for e in range(E - 1):
+            project(1, e, 1)
+        for e in range(DEPTH):
+            empty(1, e)
+            quantise_x(1, e)
+        for e in range(DEPTH):
+            expert(e)
+        for e in range(E - DEPTH):
+            add_bias(e)
+            if e < PASSES:
+                for g in range(PASSES):
+                    project(e, 5, g)
+            else:
+                empty(0, 5)
+            empty(1, e + DEPTH)
             scatter(e, 1)
+            quantise_x(1, e + DEPTH)
+            expert(e + DEPTH)
+        for e in range(E - DEPTH, E):
+            add_bias(e)
+        scatter(3, 2)
+        scatter(5, 1)
         nc.sync.dma_start(out=out, in_=result[:])

@@ -316,8 +316,13 @@ def tile_moe_prv_lin_bias_kernel(tc, uT, wu, w_words, w_scales, b, gate, offs, o
         for n in range(2):
             for pair in PAIRS:
                 round_wu(1, 1, last_raw[n], 64 * n, slice(0, 64), pair, "vector")
-        for pair in PAIRS:
-            quantise_wu(1, 1, pair)
+            for r in range(PACK):
+                words = slice(r % 2 * P + 64 * n, r % 2 * P + 64 * (n + 1))
+                nc.vector.quantize_mx(
+                    out=wu_codes[1, 1, r - r % 2][:, words].bitcast(FP8X4),
+                    scales=wu_scale[1, 1, r - r % 2][:, words],
+                    in_=wu_stage[1, 1, r - r % 2][:, words.start * PACK : words.stop * PACK],
+                )
         quantise_x(0, 3)
         quantise_x(0, 4)
         for e in range(E - 1):

@@ -24,12 +24,16 @@ S = E * C
 PER_COLUMN = 16
 WINDOW = 1024
 DEPTH = 3
-STAGE = 2 * PASS * 2
-RING = 8 * STAGE
-EVERY = slice(0, 4)
-PLACE = {(0, 0, 0): 10, (1, 0, 0): 24, (0, 1, 0): 28, (0, 1, 2): 26, (1, 1, 0): 0, (1, 1, 2): 2}
+AHEAD = 5
 EARLY, LATE = slice(0, 512), slice(512, S)
+EVERY = slice(0, 4)
 PAIRS = (slice(0, 2), slice(2, 4))
+LOW, HIGH = slice(0, 64), slice(64, P)
+EARLY_STAGE_AT, FIRST_STAGE_AT, LATE_STAGE_AT = 1024, 4096, 5120
+LAST_RAW_AT = 8192
+RING_AT, RING_STEP = 12288, 1024
+LEAD_STAGE_AT = 16384
+SECOND_STAGE_AT = 20480
 
 
 def tile_moe_prv_lin_bias_kernel(tc, uT, wu, w_words, w_scales, b, gate, offs, out):
@@ -40,60 +44,51 @@ def tile_moe_prv_lin_bias_kernel(tc, uT, wu, w_words, w_scales, b, gate, offs, o
         psum = ctx.enter_context(tc.psum_pool(name="psum", bufs=1))
         banks = [psum.tile([P, PACK, C], F32, name="bank%d" % i) for i in range(8)]
 
+        def place(shape, dtype, name, at=None):
+            if at is None:
+                return keep.tile(shape, dtype, name=name, align_bytes=64)
+            return shared.tile(shape, dtype, name=name, offset=at, align_bytes=64)
+
         def bank_of(a, e):
-            return banks[((0, 1, 2, 3, 4, 2), (5, 6, 7, 0, 1, 3))[a][e]]
+            return banks[((0, 1, 2, 3, 4, 5), (6, 7, 0, 1, 2, 3))[a][e]]
 
         def sum_bank(e):
-            return banks[e + 2]
+            return banks[(e + 3) % 8]
+
+        def columns(e):
+            return slice(e * C, (e + 1) * C)
 
         offsets = keep.tile([P, S // PER_COLUMN], U16, name="offsets")
-
-        def slots(cut):
-            return offsets[:, cut.start // PER_COLUMN : cut.stop // PER_COLUMN]
 
         u_rows = uT.rearrange("(g p h i) t -> g h p i t", g=PASSES, p=P, h=2)
         u_raw = {}
         for n in range(2):
-            u_raw[0, 0, n] = keep.tile([P, 2, T // 2], F32, name="u_first%d" % n)
+            u_raw[0, 0, n] = place([P, 2, T // 2], F32, "u_first%d" % n)
             nc.sync.dma_start(out=u_raw[0, 0, n][:], in_=u_rows[0, 0][:, :, n * T // 2 : (n + 1) * T // 2])
         nc.sync.dma_start(offsets[:], offs)
         for g, h in ((0, 1), (1, 0), (1, 1)):
-            u_raw[g, h, 0] = keep.tile([P, 2, T], F32, name="u_raw%d%d" % (g, h))
+            u_raw[g, h, 0] = place([P, 2, T], F32, "u_raw%d%d" % (g, h))
             nc.sync.dma_start(out=u_raw[g, h, 0][:], in_=u_rows[g, h])
         wu_rows = wu.rearrange("(g p j) (a c) -> g a p j c", g=PASSES, p=P, a=PASSES)
         wu_raw = {}
-        for g, a in ((0, 0), (1, 0), (0, 1)):
-            if a == 1:
-                wu_raw[g, a] = shared.tile([P, PACK, PASS], F32, name="wu_raw%d%d" % (g, a), offset=0, align_bytes=64)
-            else:
-                wu_raw[g, a] = keep.tile([P, PACK, PASS], F32, name="wu_raw%d%d" % (g, a))
-            nc.sync.dma_start(out=wu_raw[g, a][:], in_=wu_rows[g, a])
-        last_raw = []
-        for n in range(2):
-            last_raw.append(keep.tile([P, PACK, PASS // 2], F32, name="last_raw%d" % n))
-            nc.sync.dma_start(out=last_raw[n][:], in_=wu_rows[1, 1][:, :, n * 256 : (n + 1) * 256])
+        for g, a, ms in ((0, 0, slice(0, P)), (1, 0, slice(0, P)), (0, 1, slice(0, P)), (1, 1, LOW), (1, 1, HIGH)):
+            at = LAST_RAW_AT if (g, a, ms) == (1, 1, HIGH) else None
+            tile = place([P, PACK, (ms.stop - ms.start) * PACK], F32, "wu_raw%d%d_%d" % (g, a, ms.start), at)
+            nc.sync.dma_start(out=tile[:], in_=wu_rows[g, a][:, :, ms.start * PACK : ms.stop * PACK])
+            wu_raw[g, a, ms.start] = tile
 
-        w_src = w_words.rearrange("e a p n r -> p (e a) (n r)")
-        w_codes = {}
+        bias = place([P, E], F32, "bias")
+        nc.sync.dma_start(out=bias[:], in_=b)
         gate_tiles = {}
 
-        def load_words(first, count):
-            tile = keep.tile([P, count * PASSES, N * PACK], U8, name="w_codes%d" % first, align_bytes=64)
-            nc.sync.dma_start(out=tile[:].bitcast(I32), in_=w_src[:, first * PASSES : (first + count) * PASSES].bitcast(I32))
-            for e in range(first, first + count):
-                for a in range(PASSES):
-                    w_codes[e, a] = tile[:, (e - first) * PASSES + a, :]
-
         def load_gate(first, count):
-            tile = keep.tile([P, count * C], F32, name="gate%d" % first)
+            tile = place([P, count * C], F32, "gate%d" % first)
             nc.sync.dma_start(out=tile[:], in_=gate[:, first * C : (first + count) * C])
-            gate_tiles[first * C] = tile
+            for e in range(first, first + count):
+                gate_tiles[e] = (tile, first)
 
-        def gates(cut):
-            first = max(start for start in gate_tiles if start <= cut.start)
-            return gate_tiles[first][:, cut.start - first : cut.stop - first]
-
-        w_scale = keep.tile([P, E * PASSES, N], U8, name="w_scale", align_bytes=64)
+        load_gate(0, 2)
+        w_scale = place([P, E * PASSES, N], U8, "w_scale")
         nc.gpsimd.memset(w_scale[:].bitcast(I32), 0)
         scale_src = w_scales.rearrange("e a q n -> q (e a) n")
         for quad in range(4):
@@ -101,49 +96,32 @@ def tile_moe_prv_lin_bias_kernel(tc, uT, wu, w_words, w_scales, b, gate, offs, o
                 out=w_scale[32 * quad : 32 * quad + 4, :, :].bitcast(I32),
                 in_=scale_src[4 * quad : 4 * quad + 4].bitcast(I32),
             )
-        bias = keep.tile([P, E], F32, name="bias")
-        nc.sync.dma_start(out=bias[:], in_=b)
-        load_gate(0, DEPTH)
-        load_words(0, E)
-        load_gate(DEPTH, E - DEPTH)
-
-        def parts(g, a):
-            return (EVERY,) if a == 0 else PAIRS
-
-        wu_codes, wu_scale, wu_stage = {}, {}, {}
-        for a in range(PASSES):
-            for g in range(PASSES):
-                for rs in parts(g, a):
-                    n, count = rs.start, rs.stop - rs.start
-                    if (g, a, n) == (1, 1, 2):
-                        wu_codes[g, a, n] = shared.tile([P, count * P], U32, name="wu_codes_last", offset=RING + STAGE, align_bytes=64)
-                    else:
-                        wu_codes[g, a, n] = keep.tile([P, count * P], U32, name="wu_codes%d%d%d" % (g, a, n), align_bytes=64)
-                    wu_scale[g, a, n] = keep.tile([P, count * P], U8, name="wu_scale%d%d%d" % (g, a, n), align_bytes=64)
-                    wu_stage[g, a, n] = shared.tile(
-                        [P, count * PASS], BF16, name="wu_stage%d%d%d" % (g, a, n), offset=PLACE[g, a, n] * STAGE // 2, align_bytes=64
-                    )
-
-        u_codes = [keep.tile([P, S], U32, name="u_codes%d" % g, align_bytes=64) for g in range(PASSES)]
-        u_scale = [keep.tile([P, S], U8, name="u_scale%d" % g, align_bytes=64) for g in range(PASSES)]
-        late_scale = shared.tile([P, S - LATE.start], U8, name="late_scale", offset=12 * STAGE, align_bytes=64)
-
-        def u_plane(g, cut):
-            if g == 1 and cut.start >= LATE.start:
-                return late_scale[:, cut.start - LATE.start : cut.stop - LATE.start]
-            return u_scale[g][:, cut]
-
-        u_stage = [
-            keep.tile([P, S * PACK], BF16, name="u_stage0", align_bytes=64),
-            shared.tile([P, S * PACK], BF16, name="u_stage1", offset=5 * STAGE, align_bytes=64),
-        ]
+        w_src = w_words.rearrange("e a p n r -> p (e a) (n r)")
+        w_codes = {}
+        for first in range(0, E, 2):
+            tile = place([P, 2 * PASSES, N * PACK], U8, "w_codes%d" % first)
+            nc.sync.dma_start(out=tile[:].bitcast(I32), in_=w_src[:, first * PASSES : (first + 2) * PASSES].bitcast(I32))
+            for n in range(2 * PASSES):
+                w_codes[first + n // PASSES, n % PASSES] = tile[:, n, :]
+        load_gate(2, E - 2)
 
         pairs = {}
         for g in range(PASSES):
             for h in range(2):
-                pairs[g, h] = keep.tile([P, WINDOW, 2], BF16, name="pairs%d%d" % (g, h))
+                pairs[g, h] = place([P, WINDOW, 2], BF16, "pairs%d%d" % (g, h))
                 nc.gpsimd.memset(pairs[g, h][:, T:, :].rearrange("p t i -> p (t i)").bitcast(U32), 0)
-        picked = [keep.tile([P, 2, S], U32, name="picked%d" % g) for g in range(PASSES)]
+        picked = [place([P, 2, S], U32, "picked%d" % g) for g in range(PASSES)]
+        u_stage, u_codes, u_scale = {}, {}, {}
+        first_stage = place([P, S * PACK], BF16, "u_stage0")
+        for g in range(PASSES):
+            for cut in (EARLY, LATE):
+                width, key = cut.stop - cut.start, (g, cut.start)
+                if g == 0:
+                    u_stage[key] = first_stage[:, cut.start * PACK : cut.stop * PACK]
+                else:
+                    u_stage[key] = place([P, width * PACK], BF16, "u_stage%d_%d" % key, LATE_STAGE_AT if cut == LATE else EARLY_STAGE_AT)[:]
+                u_codes[key] = place([P, width], U32, "u_codes%d_%d" % key)
+                u_scale[key] = place([P, width], U8, "u_scale%d_%d" % key, SECOND_STAGE_AT if key == (1, LATE.start) else None)
 
         def round_pairs(g, h, n, cut, engine):
             first = n * T // 2
@@ -162,16 +140,32 @@ def tile_moe_prv_lin_bias_kernel(tc, uT, wu, w_words, w_scales, b, gate, offs, o
             window = pairs[g, h][:].rearrange("p t i -> p (t i)").bitcast(U32)
             nc.vector.tensor_copy(out=picked[g][:, h, :], in_=window.indirect(offsets[:]))
 
-        def quantise_u(g, cut):
-            nc.vector.quantize_mx(
-                out=u_codes[g][:, cut].bitcast(FP8X4),
-                scales=u_plane(g, cut),
-                in_=u_stage[g][:, cut.start * PACK : cut.stop * PACK],
+        def interleave(cut):
+            nc.vector.tensor_copy(
+                out=u_stage[1, cut.start].rearrange("p (s h i) -> p s h i", h=2, i=2),
+                in_=picked[1][:].bitcast(BF16).rearrange("p h (s i) -> p s h i", i=2)[:, cut],
             )
 
-        def round_wu(g, a, raw, first, cut, pair, engine):
-            dst = wu_stage[g, a, pair.start][:].rearrange("p (r m j) -> p m j r", m=P, j=PACK)[:, first + cut.start : first + cut.stop]
-            src = raw[:].rearrange("p j (m r) -> p m j r", r=PACK)[:, cut, :, pair]
+        def quantise_u(g, cut):
+            key = (g, cut.start)
+            nc.vector.quantize_mx(out=u_codes[key][:].bitcast(FP8X4), scales=u_scale[key][:], in_=u_stage[key])
+
+        def parts(g, a):
+            return (EVERY,) if (g, a) == (1, 0) else PAIRS
+
+        wu_stage, wu_codes, wu_scale = {}, {}, {}
+        for a in range(PASSES):
+            for g in range(PASSES):
+                for rs in parts(g, a):
+                    key, count = (g, a, rs.start), rs.stop - rs.start
+                    wu_stage[key] = place([P, count * PASS], BF16, "wu_stage%d%d%d" % key, {(0, 0, 0): FIRST_STAGE_AT, (1, 0, 0): SECOND_STAGE_AT}.get(key))
+                    wu_codes[key] = place([P, count * P], U32, "wu_codes%d%d%d" % key)
+                    wu_scale[key] = place([P, count * P], U8, "wu_scale%d%d%d" % key)
+
+        def round_wu(g, a, ms, rs, engine):
+            first = max(key[2] for key in wu_raw if key[:2] == (g, a) and key[2] <= ms.start)
+            dst = wu_stage[g, a, rs.start][:].rearrange("p (r m j) -> p m j r", m=P, j=PACK)[:, ms]
+            src = wu_raw[g, a, first][:].rearrange("p j (m r) -> p m j r", r=PACK)[:, ms.start - first : ms.stop - first, :, rs]
             if engine == "vector":
                 nc.vector.tensor_copy(out=dst, in_=src)
             elif engine == "gpsimd":
@@ -180,40 +174,17 @@ def tile_moe_prv_lin_bias_kernel(tc, uT, wu, w_words, w_scales, b, gate, offs, o
             else:
                 nc.scalar.copy(out=dst, in_=src)
 
-        def quantise_wu(g, a, rs):
+        def quantise_wu(g, a, rs, words):
+            key = (g, a, rs.start)
             nc.vector.quantize_mx(
-                out=wu_codes[g, a, rs.start][:].bitcast(FP8X4),
-                scales=wu_scale[g, a, rs.start][:],
-                in_=wu_stage[g, a, rs.start][:],
+                out=wu_codes[key][:, words].bitcast(FP8X4),
+                scales=wu_scale[key][:, words],
+                in_=wu_stage[key][:, words.start * PACK : words.stop * PACK],
             )
 
-        x_stage, x_codes, x_scale = {}, {}, {}
-        groups = [[(0, e) for e in range(4)]] + [[(0, 4)]] + [[(1, e)] for e in range(5)] + [[(0, 5), (1, 5)]]
-        group_tiles = {}
-        for n, group in enumerate(groups):
-            width = len(group) * C
-            if group in ([(1, DEPTH)], [(1, DEPTH + 1)]):
-                stage = shared.tile([P, width * PACK], BF16, name="x_stage%d" % n, offset=RING + 1024 * (group[0][1] - DEPTH), align_bytes=64)
-            else:
-                stage = keep.tile([P, width * PACK], BF16, name="x_stage%d" % n, align_bytes=64)
-            if group in ([(1, 0)], [(1, 1)]):
-                codes = shared.tile([P, width], U32, name="x_codes%d" % n, offset=RING + 1024 * group[0][1], align_bytes=64)
-            else:
-                codes = keep.tile([P, width], U32, name="x_codes%d" % n, align_bytes=64)
-            if n < 2:
-                scale = shared.tile([P, width], U8, name="x_scale%d" % n, offset=512 * n, align_bytes=64)
-            else:
-                scale = keep.tile([P, width], U8, name="x_scale%d" % n, align_bytes=64)
-            group_tiles[group[-1]] = (stage, codes, scale)
-            for i, key in enumerate(group):
-                x_stage[key] = stage[:, i * C * PACK : (i + 1) * C * PACK]
-                x_codes[key] = codes[:, i * C : (i + 1) * C]
-                x_scale[key] = scale[:, i * C : (i + 1) * C]
-
-        def columns(e):
-            return slice(e * C, (e + 1) * C)
-
         def project(a, e, g):
+            cut = EARLY if e * C < LATE.start else LATE
+            slots = slice(e * C - cut.start, (e + 1) * C - cut.start)
             order = (2, 3, 0, 1) if (g, a) == (0, 1) else (0, 1, 2, 3)
             for r in order:
                 first = max(rs.start for rs in parts(g, a) if rs.start <= r)
@@ -222,37 +193,48 @@ def tile_moe_prv_lin_bias_kernel(tc, uT, wu, w_words, w_scales, b, gate, offs, o
                     out=bank_of(a, e)[:, r, :],
                     lhsT=wu_codes[g, a, first][:, words].bitcast(FP8X4),
                     lhsT_scale=wu_scale[g, a, first][:, words],
-                    rhs=u_codes[g][:, columns(e)].bitcast(FP8X4),
-                    rhs_scale=u_plane(g, columns(e)),
+                    rhs=u_codes[g, cut.start][:, slots].bitcast(FP8X4),
+                    rhs_scale=u_scale[g, cut.start][:, slots],
                     start=(g == 0 and r == order[0]),
                     stop=(g == PASSES - 1 and r == PACK - 1),
                 )
 
+        x_stage, x_codes, x_scale, group_tiles = {}, {}, {}, {}
+        groups = [[(0, e) for e in range(4)], [(0, 4)], [(0, 5)], [(1, 0)], [(1, 1)], [(1, 2)], [(1, 3)], [(1, 4), (1, 5)]]
+        stage_at = {(0, 5): LAST_RAW_AT + 1024, (1, 0): LEAD_STAGE_AT, (1, 3): RING_AT, (1, 4): RING_AT + RING_STEP}
+        codes_at = {(1, e): RING_AT + RING_STEP * e for e in range(2)}
+        scale_at = {(0, 0): LAST_RAW_AT, (0, 4): LAST_RAW_AT + 512, (0, 5): LEAD_STAGE_AT}
+        for n, group in enumerate(groups):
+            width = len(group) * C
+            stage = place([P, width * PACK], BF16, "x_stage%d" % n, stage_at.get(group[0]))
+            codes = place([P, width], U32, "x_codes%d" % n, codes_at.get(group[0]))
+            scale = place([P, width], U8, "x_scale%d" % n, scale_at.get(group[0]))
+            group_tiles[group[-1]] = (stage, codes, scale)
+            for i, key in enumerate(group):
+                x_stage[key] = stage[:, i * C * PACK : (i + 1) * C * PACK]
+                x_codes[key] = codes[:, i * C : (i + 1) * C]
+                x_scale[key] = scale[:, i * C : (i + 1) * C]
+
         def empty(a, e):
-            nc.scalar.copy(
-                out=x_stage[a, e].rearrange("p (s r) -> p s r", r=PACK),
-                in_=bank_of(a, e)[:].rearrange("p r s -> p s r"),
-            )
+            dst = x_stage[a, e].rearrange("p (s r) -> p s r", r=PACK)
+            src = bank_of(a, e)[:].rearrange("p r s -> p s r")
+            if (a, e) == (0, E - 1):
+                nc.vector.tensor_copy(out=dst, in_=src)
+            else:
+                nc.scalar.copy(out=dst, in_=src)
 
         def quantise_x(a, e):
             stage, codes, scale = group_tiles[a, e]
             nc.vector.quantize_mx(out=codes[:].bitcast(FP8X4), scales=scale[:], in_=stage[:])
 
-        y = keep.tile([P, S], F32, name="y")
-        y_late = shared.tile([P, 2 * C], F32, name="y_late", offset=RING + STAGE, align_bytes=64)
-
-        def sums(cut):
-            if cut.start in (3 * C, 4 * C):
-                return y_late[:, cut.start - 3 * C : cut.stop - 3 * C]
-            return y[:, cut]
-
+        sum_tiles = {e: place([P, count * C], F32, "sums%d" % e) for e, count in ((0, 1), (1, 1), (2, 2), (4, 2))}
+        sums = [sum_tiles[0], sum_tiles[1], sum_tiles[2][:, :C], sum_tiles[2][:, C:], sum_tiles[4][:, :C], sum_tiles[4][:, C:]]
         result = keep.tile([P, T], F32, name="result")
 
         def expert(e):
-            acc = sum_bank(e)[:, 0, :]
             for a in range(PASSES):
                 nc.tensor.matmul_mx(
-                    out=acc,
+                    out=sum_bank(e)[:, 0, :],
                     lhsT=w_codes[e, a].bitcast(FP8X4),
                     lhsT_scale=w_scale[:, e * PASSES + a, :],
                     rhs=x_codes[a, e].bitcast(FP8X4),
@@ -262,15 +244,14 @@ def tile_moe_prv_lin_bias_kernel(tc, uT, wu, w_words, w_scales, b, gate, offs, o
                 )
 
         def add_bias(e):
-            nc.scalar.activation(sums(columns(e)), sum_bank(e)[:, 0, :], IDENTITY, bias=bias[:, e : e + 1])
+            nc.scalar.activation(sums[e][:], sum_bank(e)[:, 0, :], IDENTITY, bias=bias[:, e : e + 1])
 
-        def scatter(first, count):
-            cut = slice(first * C, (first + count) * C)
-            nc.vector.tensor_tensor(result[:].indirect(slots(cut)), sums(cut), gates(cut), MULT)
+        def scatter(e, count):
+            slots = offsets[:, e * C // PER_COLUMN : (e + count) * C // PER_COLUMN]
+            tile, first = gate_tiles[e]
+            nc.vector.tensor_tensor(result[:].indirect(slots), sum_tiles[e][:], tile[:, (e - first) * C : (e - first + count) * C], MULT)
 
-        half, whole = slice(0, T // 2), slice(0, P)
-
-        round_pairs(0, 0, 0, half, "vector")
+        round_pairs(0, 0, 0, slice(0, T // 2), "vector")
         round_pairs(0, 0, 1, slice(0, 256), "vector")
         round_pairs(0, 0, 1, slice(256, 384), "scalar")
         gather(0, 0)
@@ -281,7 +262,7 @@ def tile_moe_prv_lin_bias_kernel(tc, uT, wu, w_words, w_scales, b, gate, offs, o
         round_pairs(1, 0, 0, slice(320, T), "scalar")
         gather(1, 0)
         nc.scalar.copy(
-            out=u_stage[0][:].bitcast(U32).rearrange("p (s h) -> p s h", h=2),
+            out=first_stage[:].bitcast(U32).rearrange("p (s h) -> p s h", h=2),
             in_=picked[0][:].rearrange("p h s -> p s h"),
         )
         round_pairs(1, 1, 0, slice(0, 448), "gpsimd")
@@ -289,62 +270,61 @@ def tile_moe_prv_lin_bias_kernel(tc, uT, wu, w_words, w_scales, b, gate, offs, o
         for cut in (EARLY, LATE):
             quantise_u(0, cut)
         gather(1, 1)
-        round_wu(0, 0, wu_raw[0, 0], 0, slice(0, 48), EVERY, "gpsimd")
-        round_wu(0, 0, wu_raw[0, 0], 0, slice(48, P), EVERY, "scalar")
-        quantise_wu(0, 0, EVERY)
-        for cut in (EARLY, LATE):
-            nc.vector.tensor_copy(
-                out=u_stage[1][:].rearrange("p (s h i) -> p s h i", h=2, i=2)[:, cut],
-                in_=picked[1][:].bitcast(BF16).rearrange("p h (s i) -> p s h i", i=2)[:, cut],
-            )
-        round_wu(1, 0, wu_raw[1, 0], 0, slice(0, 24), EVERY, "vector")
-        round_wu(1, 0, wu_raw[1, 0], 0, slice(24, P), EVERY, "scalar")
+        round_wu(0, 0, slice(0, 96), PAIRS[1], "gpsimd")
+        round_wu(0, 0, slice(0, P), PAIRS[0], "scalar")
+        round_wu(0, 0, slice(96, P), PAIRS[1], "scalar")
+        for rs in PAIRS:
+            quantise_wu(0, 0, rs, slice(0, 2 * P))
+        interleave(EARLY)
+        interleave(LATE)
         quantise_u(1, EARLY)
-        for e in range(E - 1):
+        round_wu(1, 0, slice(0, 32), EVERY, "vector")
+        round_wu(1, 0, slice(32, P), EVERY, "scalar")
+        for e in range(E):
             project(0, e, 0)
-        quantise_wu(1, 0, EVERY)
-        round_wu(0, 1, wu_raw[0, 1], 0, whole, PAIRS[0], "scalar")
-        round_wu(0, 1, wu_raw[0, 1], 0, whole, PAIRS[1], "vector")
+        quantise_wu(1, 0, EVERY, slice(0, PASS))
+        round_wu(0, 1, slice(0, P), PAIRS[0], "scalar")
+        round_wu(0, 1, slice(0, P), PAIRS[1], "vector")
         quantise_u(1, LATE)
-        for e in range(E - 1):
+        for e in range(E):
             project(0, e, 1)
-            empty(0, e)
-        for pair in reversed(PAIRS):
-            quantise_wu(0, 1, pair)
-        for e in range(E - 1):
+            if e < E - 1:
+                empty(0, e)
+        for rs in reversed(PAIRS):
+            quantise_wu(0, 1, rs, slice(0, 2 * P))
+        for e in range(AHEAD):
             project(1, e, 0)
-        for n in range(2):
-            for pair in PAIRS:
-                round_wu(1, 1, last_raw[n], 64 * n, slice(0, 64), pair, "vector")
-            for r in range(PACK):
-                words = slice(r % 2 * P + 64 * n, r % 2 * P + 64 * (n + 1))
-                nc.vector.quantize_mx(
-                    out=wu_codes[1, 1, r - r % 2][:, words].bitcast(FP8X4),
-                    scales=wu_scale[1, 1, r - r % 2][:, words],
-                    in_=wu_stage[1, 1, r - r % 2][:, words.start * PACK : words.stop * PACK],
-                )
+        for ms in (LOW, HIGH):
+            for rs in PAIRS:
+                round_wu(1, 1, ms, rs, "vector")
+            for rs in PAIRS:
+                for r in range(2):
+                    quantise_wu(1, 1, rs, slice(r * P + ms.start, r * P + ms.stop))
+        empty(0, 5)
         quantise_x(0, 3)
         quantise_x(0, 4)
-        for e in range(E - 1):
+        for e in range(AHEAD):
             project(1, e, 1)
         for e in range(DEPTH):
             empty(1, e)
             quantise_x(1, e)
-        for e in range(DEPTH):
+            if e == 0:
+                quantise_x(0, 5)
+        for e in range(2):
             expert(e)
-        for e in range(E - DEPTH):
             add_bias(e)
-            if e < PASSES:
-                for g in range(PASSES):
-                    project(e, 5, g)
-            else:
-                empty(0, 5)
-            empty(1, e + DEPTH)
             scatter(e, 1)
-            quantise_x(1, e + DEPTH)
-            expert(e + DEPTH)
-        for e in range(E - DEPTH, E):
+            if e == 0:
+                for g in range(PASSES):
+                    project(1, E - 1, g)
+                empty(1, 3)
+                quantise_x(1, 3)
+        empty(1, 4)
+        empty(1, 5)
+        quantise_x(1, 5)
+        for e in range(2, E):
+            expert(e)
             add_bias(e)
-        scatter(3, 2)
-        scatter(5, 1)
+            if e % 2:
+                scatter(e - 1, 2)
         nc.sync.dma_start(out=out, in_=result[:])

@@ -46,8 +46,8 @@ def tile_moe_prv_lin_bias_kernel(tc, uT, wu, w_words, w_scales, b, gate, offs, o
 
         def place(shape, dtype, name, at=None):
             if at is None:
-                return keep.tile(shape, dtype, name=name, align_bytes=64)
-            return shared.tile(shape, dtype, name=name, offset=at, align_bytes=64)
+                return keep.tile(shape, dtype, name=name, align_bytes=256)
+            return shared.tile(shape, dtype, name=name, offset=at, align_bytes=256)
 
         def bank_of(a, e):
             return banks[((0, 1, 2, 3, 4, 5), (6, 7, 0, 1, 2, 3))[a][e]]
@@ -229,7 +229,7 @@ def tile_moe_prv_lin_bias_kernel(tc, uT, wu, w_words, w_scales, b, gate, offs, o
 
         sum_tiles = {e: place([P, count * C], F32, "sums%d" % e) for e, count in ((0, 1), (1, 1), (2, 2), (4, 2))}
         sums = [sum_tiles[0], sum_tiles[1], sum_tiles[2][:, :C], sum_tiles[2][:, C:], sum_tiles[4][:, :C], sum_tiles[4][:, C:]]
-        result = keep.tile([P, T], F32, name="result")
+        result = place([P, T], F32, "result")
 
         def expert(e):
             for a in range(PASSES):

@@ -29,11 +29,13 @@ EARLY, LATE = slice(0, 512), slice(512, S)
 EVERY = slice(0, 4)
 PAIRS = (slice(0, 2), slice(2, 4))
 LOW, HIGH = slice(0, 64), slice(64, P)
-EARLY_STAGE_AT, FIRST_STAGE_AT, LATE_STAGE_AT = 1024, 4096, 5120
-LAST_RAW_AT = 8192
+LAST_TOKENS_AT = 0
+PICKED_AT = 6144
 RING_AT, RING_STEP = 12288, 1024
 LEAD_STAGE_AT = 16384
-SECOND_STAGE_AT = 20480
+LAST_RAW_AT = 20480
+SECOND_RAW_AT = 24576
+THIRD_RAW_AT = 32768
 
 
 def tile_moe_prv_lin_bias_kernel(tc, uT, wu, w_words, w_scales, b, gate, offs, out):
@@ -67,12 +69,12 @@ def tile_moe_prv_lin_bias_kernel(tc, uT, wu, w_words, w_scales, b, gate, offs, o
             nc.sync.dma_start(out=u_raw[0, 0, n][:], in_=u_rows[0, 0][:, :, n * T // 2 : (n + 1) * T // 2])
         nc.sync.dma_start(offsets[:], offs)
         for g, h in ((0, 1), (1, 0), (1, 1)):
-            u_raw[g, h, 0] = place([P, 2, T], F32, "u_raw%d%d" % (g, h))
+            u_raw[g, h, 0] = place([P, 2, T], F32, "u_raw%d%d" % (g, h), LAST_TOKENS_AT if (g, h) == (1, 1) else None)
             nc.sync.dma_start(out=u_raw[g, h, 0][:], in_=u_rows[g, h])
         wu_rows = wu.rearrange("(g p j) (a c) -> g a p j c", g=PASSES, p=P, a=PASSES)
         wu_raw = {}
         for g, a, ms in ((0, 0, slice(0, P)), (1, 0, slice(0, P)), (0, 1, slice(0, P)), (1, 1, LOW), (1, 1, HIGH)):
-            at = LAST_RAW_AT if (g, a, ms) == (1, 1, HIGH) else None
+            at = {(1, 0, 0): SECOND_RAW_AT, (0, 1, 0): THIRD_RAW_AT, (1, 1, HIGH.start): LAST_RAW_AT}.get((g, a, ms.start))
             tile = place([P, PACK, (ms.stop - ms.start) * PACK], F32, "wu_raw%d%d_%d" % (g, a, ms.start), at)
             nc.sync.dma_start(out=tile[:], in_=wu_rows[g, a][:, :, ms.start * PACK : ms.stop * PACK])
             wu_raw[g, a, ms.start] = tile
@@ -110,18 +112,15 @@ def tile_moe_prv_lin_bias_kernel(tc, uT, wu, w_words, w_scales, b, gate, offs, o
             for h in range(2):
                 pairs[g, h] = place([P, WINDOW, 2], BF16, "pairs%d%d" % (g, h))
                 nc.gpsimd.memset(pairs[g, h][:, T:, :].rearrange("p t i -> p (t i)").bitcast(U32), 0)
-        picked = [place([P, 2, S], U32, "picked%d" % g) for g in range(PASSES)]
+        picked = [place([P, 2, S], U32, "picked%d" % g, PICKED_AT if g == 0 else None) for g in range(PASSES)]
         u_stage, u_codes, u_scale = {}, {}, {}
-        first_stage = place([P, S * PACK], BF16, "u_stage0")
+        token_stage_at = {(0, EARLY.start): LAST_TOKENS_AT, (1, EARLY.start): PICKED_AT, (1, LATE.start): SECOND_RAW_AT}
         for g in range(PASSES):
             for cut in (EARLY, LATE):
                 width, key = cut.stop - cut.start, (g, cut.start)
-                if g == 0:
-                    u_stage[key] = first_stage[:, cut.start * PACK : cut.stop * PACK]
-                else:
-                    u_stage[key] = place([P, width * PACK], BF16, "u_stage%d_%d" % key, LATE_STAGE_AT if cut == LATE else EARLY_STAGE_AT)[:]
+                u_stage[key] = place([P, width * PACK], BF16, "u_stage%d_%d" % key, token_stage_at.get(key))
                 u_codes[key] = place([P, width], U32, "u_codes%d_%d" % key)
-                u_scale[key] = place([P, width], U8, "u_scale%d_%d" % key, SECOND_STAGE_AT if key == (1, LATE.start) else None)
+                u_scale[key] = place([P, width], U8, "u_scale%d_%d" % key, SECOND_RAW_AT + 2048 if key == (0, LATE.start) else None)
 
         def round_pairs(g, h, n, cut, engine):
             first = n * T // 2
@@ -140,25 +139,36 @@ def tile_moe_prv_lin_bias_kernel(tc, uT, wu, w_words, w_scales, b, gate, offs, o
             window = pairs[g, h][:].rearrange("p t i -> p (t i)").bitcast(U32)
             nc.vector.tensor_copy(out=picked[g][:, h, :], in_=window.indirect(offsets[:]))
 
-        def interleave(cut):
-            nc.vector.tensor_copy(
-                out=u_stage[1, cut.start].rearrange("p (s h i) -> p s h i", h=2, i=2),
-                in_=picked[1][:].bitcast(BF16).rearrange("p h (s i) -> p s h i", i=2)[:, cut],
+        def interleave(g, cut, engine):
+            stage = u_stage[g, cut.start][:]
+            if engine == "vector":
+                nc.vector.tensor_copy(
+                    out=stage.rearrange("p (s h i) -> p s h i", h=2, i=2),
+                    in_=picked[g][:].bitcast(BF16).rearrange("p h (s i) -> p s h i", i=2)[:, cut],
+                )
+            else:
+                nc.scalar.copy(
+                    out=stage.bitcast(U32).rearrange("p (s h) -> p s h", h=2),
+                    in_=picked[g][:].rearrange("p h s -> p s h")[:, cut],
+                )
+
+        def quantise_u(g, cut, words):
+            key = (g, cut.start)
+            nc.vector.quantize_mx(
+                out=u_codes[key][:, words].bitcast(FP8X4),
+                scales=u_scale[key][:, words],
+                in_=u_stage[key][:, words.start * PACK : words.stop * PACK],
             )
 
-        def quantise_u(g, cut):
-            key = (g, cut.start)
-            nc.vector.quantize_mx(out=u_codes[key][:].bitcast(FP8X4), scales=u_scale[key][:], in_=u_stage[key])
-
         def parts(g, a):
-            return (EVERY,) if (g, a) == (1, 0) else PAIRS
+            return PAIRS
 
         wu_stage, wu_codes, wu_scale = {}, {}, {}
         for a in range(PASSES):
             for g in range(PASSES):
                 for rs in parts(g, a):
                     key, count = (g, a, rs.start), rs.stop - rs.start
-                    wu_stage[key] = place([P, count * PASS], BF16, "wu_stage%d%d%d" % key, {(0, 0, 0): FIRST_STAGE_AT, (1, 0, 0): SECOND_STAGE_AT}.get(key))
+                    wu_stage[key] = place([P, count * PASS], BF16, "wu_stage%d%d%d" % key)
                     wu_codes[key] = place([P, count * P], U32, "wu_codes%d%d%d" % key)
                     wu_scale[key] = place([P, count * P], U8, "wu_scale%d%d%d" % key)
 
@@ -185,7 +195,7 @@ def tile_moe_prv_lin_bias_kernel(tc, uT, wu, w_words, w_scales, b, gate, offs, o
         def project(a, e, g):
             cut = EARLY if e * C < LATE.start else LATE
             slots = slice(e * C - cut.start, (e + 1) * C - cut.start)
-            order = (2, 3, 0, 1) if (g, a) == (0, 1) else (0, 1, 2, 3)
+            order = (0, 1, 2, 3)
             for r in order:
                 first = max(rs.start for rs in parts(g, a) if rs.start <= r)
                 words = slice((r - first) * P, (r - first + 1) * P)
@@ -201,7 +211,7 @@ def tile_moe_prv_lin_bias_kernel(tc, uT, wu, w_words, w_scales, b, gate, offs, o
 
         x_stage, x_codes, x_scale, group_tiles = {}, {}, {}, {}
         groups = [[(0, e) for e in range(4)], [(0, 4)], [(0, 5)], [(1, 0)], [(1, 1)], [(1, 2)], [(1, 3)], [(1, 4), (1, 5)]]
-        stage_at = {(0, 5): LAST_RAW_AT + 1024, (1, 0): LEAD_STAGE_AT, (1, 3): RING_AT, (1, 4): RING_AT + RING_STEP}
+        stage_at = {(0, 0): THIRD_RAW_AT, (0, 5): LAST_RAW_AT + 1024, (1, 0): LEAD_STAGE_AT, (1, 3): RING_AT, (1, 4): RING_AT + RING_STEP}
         codes_at = {(1, e): RING_AT + RING_STEP * e for e in range(2)}
         scale_at = {(0, 0): LAST_RAW_AT, (0, 4): LAST_RAW_AT + 512, (0, 5): LEAD_STAGE_AT}
         for n, group in enumerate(groups):
@@ -261,37 +271,41 @@ def tile_moe_prv_lin_bias_kernel(tc, uT, wu, w_words, w_scales, b, gate, offs, o
         round_pairs(1, 0, 0, slice(0, 320), "gpsimd")
         round_pairs(1, 0, 0, slice(320, T), "scalar")
         gather(1, 0)
-        nc.scalar.copy(
-            out=first_stage[:].bitcast(U32).rearrange("p (s h) -> p s h", h=2),
-            in_=picked[0][:].rearrange("p h s -> p s h"),
-        )
-        round_pairs(1, 1, 0, slice(0, 448), "gpsimd")
-        round_pairs(1, 1, 0, slice(448, T), "scalar")
-        for cut in (EARLY, LATE):
-            quantise_u(0, cut)
+        interleave(0, LATE, "scalar")
+        round_pairs(1, 1, 0, slice(0, 432), "gpsimd")
+        round_pairs(1, 1, 0, slice(432, T), "scalar")
         gather(1, 1)
-        round_wu(0, 0, slice(0, 96), PAIRS[1], "gpsimd")
-        round_wu(0, 0, slice(0, P), PAIRS[0], "scalar")
-        round_wu(0, 0, slice(96, P), PAIRS[1], "scalar")
+        interleave(0, EARLY, "scalar")
+        quantise_u(0, EARLY, slice(0, 256))
+        interleave(1, EARLY, "vector")
+        quantise_u(0, EARLY, slice(256, 512))
+        for rs in PAIRS:
+            round_wu(0, 0, slice(0, P), rs, "scalar")
+        quantise_u(1, EARLY, slice(0, 512))
         for rs in PAIRS:
             quantise_wu(0, 0, rs, slice(0, 2 * P))
-        interleave(EARLY)
-        interleave(LATE)
-        quantise_u(1, EARLY)
-        round_wu(1, 0, slice(0, 32), EVERY, "vector")
-        round_wu(1, 0, slice(32, P), EVERY, "scalar")
-        for e in range(E):
+        for e in range(4):
             project(0, e, 0)
-        quantise_wu(1, 0, EVERY, slice(0, PASS))
-        round_wu(0, 1, slice(0, P), PAIRS[0], "scalar")
-        round_wu(0, 1, slice(0, P), PAIRS[1], "vector")
-        quantise_u(1, LATE)
-        for e in range(E):
+        for rs in PAIRS:
+            round_wu(1, 0, LOW, rs, "vector")
+            round_wu(1, 0, HIGH, rs, "scalar")
+        for rs in PAIRS:
+            quantise_wu(1, 0, rs, slice(0, 2 * P))
+        for e in range(4):
             project(0, e, 1)
-            if e < E - 1:
-                empty(0, e)
-        for rs in reversed(PAIRS):
+        interleave(1, LATE, "scalar")
+        for g in range(PASSES):
+            quantise_u(g, LATE, slice(0, 256))
+        for e in range(4, E):
+            for g in range(PASSES):
+                project(0, e, g)
+        for rs in PAIRS:
+            round_wu(0, 1, slice(0, 80), rs, "vector")
+            round_wu(0, 1, slice(80, P), rs, "scalar")
+        for rs in PAIRS:
             quantise_wu(0, 1, rs, slice(0, 2 * P))
+        for e in range(E - 1):
+            empty(0, e)
         for e in range(AHEAD):
             project(1, e, 0)
         for ms in (LOW, HIGH):

@@ -25,6 +25,7 @@ PER_COLUMN = 16
 WINDOW = 1024
 DEPTH = 3
 AHEAD = 5
+WARM_UP = 5
 EARLY, LATE = slice(0, 512), slice(512, S)
 EVERY = slice(0, 4)
 PAIRS = (slice(0, 2), slice(2, 4))
@@ -277,6 +278,16 @@ def tile_moe_prv_lin_bias_kernel(tc, uT, wu, w_words, w_scales, b, gate, offs, o
         gather(1, 1)
         interleave(0, EARLY, "scalar")
         quantise_u(0, EARLY, slice(0, 256))
+        for n in range(WARM_UP):
+            nc.tensor.matmul_mx(
+                out=banks[7][:, :2, :].rearrange("p r s -> p (r s)"),
+                lhsT=u_codes[0, 0][:, :P].bitcast(FP8X4),
+                lhsT_scale=u_scale[0, 0][:, :P],
+                rhs=u_codes[0, 0][:, : 2 * P].bitcast(FP8X4),
+                rhs_scale=u_scale[0, 0][:, : 2 * P],
+                start=True,
+                stop=True,
+            )
         interleave(1, EARLY, "vector")
         quantise_u(0, EARLY, slice(256, 512))
         for rs in PAIRS:

@@ -37,6 +37,7 @@ LEAD_STAGE_AT = 16384
 LAST_RAW_AT = 20480
 SECOND_RAW_AT = 24576
 THIRD_RAW_AT = 32768
+FIRST_RAW_AT = 40960
 
 
 def tile_moe_prv_lin_bias_kernel(tc, uT, wu, w_words, w_scales, b, gate, offs, out):
@@ -65,17 +66,15 @@ def tile_moe_prv_lin_bias_kernel(tc, uT, wu, w_words, w_scales, b, gate, offs, o
 
         u_rows = uT.rearrange("(g p h i) t -> g h p i t", g=PASSES, p=P, h=2)
         u_raw = {}
-        for n in range(2):
-            u_raw[0, 0, n] = place([P, 2, T // 2], F32, "u_first%d" % n)
-            nc.sync.dma_start(out=u_raw[0, 0, n][:], in_=u_rows[0, 0][:, :, n * T // 2 : (n + 1) * T // 2])
-        nc.sync.dma_start(offsets[:], offs)
-        for g, h in ((0, 1), (1, 0), (1, 1)):
+        for g, h in ((0, 0), (0, 1), (1, 0), (1, 1)):
             u_raw[g, h, 0] = place([P, 2, T], F32, "u_raw%d%d" % (g, h), LAST_TOKENS_AT if (g, h) == (1, 1) else None)
             nc.sync.dma_start(out=u_raw[g, h, 0][:], in_=u_rows[g, h])
+            if (g, h) == (0, 0):
+                nc.sync.dma_start(offsets[:], offs)
         wu_rows = wu.rearrange("(g p j) (a c) -> g a p j c", g=PASSES, p=P, a=PASSES)
         wu_raw = {}
         for g, a, ms in ((0, 0, slice(0, P)), (1, 0, slice(0, P)), (0, 1, slice(0, P)), (1, 1, LOW), (1, 1, HIGH)):
-            at = {(1, 0, 0): SECOND_RAW_AT, (0, 1, 0): THIRD_RAW_AT, (1, 1, HIGH.start): LAST_RAW_AT}.get((g, a, ms.start))
+            at = {(0, 0, 0): FIRST_RAW_AT, (1, 0, 0): SECOND_RAW_AT, (0, 1, 0): THIRD_RAW_AT, (1, 1, HIGH.start): LAST_RAW_AT}.get((g, a, ms.start))
             tile = place([P, PACK, (ms.stop - ms.start) * PACK], F32, "wu_raw%d%d_%d" % (g, a, ms.start), at)
             nc.sync.dma_start(out=tile[:], in_=wu_rows[g, a][:, :, ms.start * PACK : ms.stop * PACK])
             wu_raw[g, a, ms.start] = tile
@@ -115,7 +114,7 @@ def tile_moe_prv_lin_bias_kernel(tc, uT, wu, w_words, w_scales, b, gate, offs, o
                 nc.gpsimd.memset(pairs[g, h][:, T:, :].rearrange("p t i -> p (t i)").bitcast(U32), 0)
         picked = [place([P, 2, S], U32, "picked%d" % g, PICKED_AT if g == 0 else None) for g in range(PASSES)]
         u_stage, u_codes, u_scale = {}, {}, {}
-        token_stage_at = {(0, EARLY.start): LAST_TOKENS_AT, (1, EARLY.start): PICKED_AT, (1, LATE.start): SECOND_RAW_AT}
+        token_stage_at = {(0, EARLY.start): LAST_TOKENS_AT, (1, EARLY.start): PICKED_AT, (1, LATE.start): FIRST_RAW_AT}
         for g in range(PASSES):
             for cut in (EARLY, LATE):
                 width, key = cut.stop - cut.start, (g, cut.start)
@@ -262,9 +261,8 @@ def tile_moe_prv_lin_bias_kernel(tc, uT, wu, w_words, w_scales, b, gate, offs, o
             tile, first = gate_tiles[e]
             nc.vector.tensor_tensor(result[:].indirect(slots), sum_tiles[e][:], tile[:, (e - first) * C : (e - first + count) * C], MULT)
 
-        round_pairs(0, 0, 0, slice(0, T // 2), "vector")
-        round_pairs(0, 0, 1, slice(0, 256), "vector")
-        round_pairs(0, 0, 1, slice(256, 384), "scalar")
+        round_pairs(0, 0, 0, slice(0, 528), "vector")
+        round_pairs(0, 0, 0, slice(528, T), "scalar")
         gather(0, 0)
         round_pairs(0, 1, 0, slice(0, 320), "gpsimd")
         round_pairs(0, 1, 0, slice(320, T), "scalar")
@@ -311,8 +309,8 @@ def tile_moe_prv_lin_bias_kernel(tc, uT, wu, w_words, w_scales, b, gate, offs, o
             for g in range(PASSES):
                 project(0, e, g)
         for rs in PAIRS:
-            round_wu(0, 1, slice(0, 80), rs, "vector")
-            round_wu(0, 1, slice(80, P), rs, "scalar")
+            round_wu(0, 1, slice(0, 72), rs, "vector")
+            round_wu(0, 1, slice(72, P), rs, "scalar")
         for rs in PAIRS:
             quantise_wu(0, 1, rs, slice(0, 2 * P))
         for e in range(E - 1):

@@ -37,7 +37,7 @@ LEAD_STAGE_AT = 16384
 LAST_RAW_AT = 20480
 SECOND_RAW_AT = 24576
 THIRD_RAW_AT = 32768
-FIRST_RAW_AT = 40960
+FIRST_RAW_AT = 45056
 
 
 def tile_moe_prv_lin_bias_kernel(tc, uT, wu, w_words, w_scales, b, gate, offs, out):
@@ -211,9 +211,9 @@ def tile_moe_prv_lin_bias_kernel(tc, uT, wu, w_words, w_scales, b, gate, offs, o
 
         x_stage, x_codes, x_scale, group_tiles = {}, {}, {}, {}
         groups = [[(0, e) for e in range(4)], [(0, 4)], [(0, 5)], [(1, 0)], [(1, 1)], [(1, 2)], [(1, 3)], [(1, 4), (1, 5)]]
-        stage_at = {(0, 0): THIRD_RAW_AT, (0, 5): LAST_RAW_AT + 1024, (1, 0): LEAD_STAGE_AT, (1, 3): RING_AT, (1, 4): RING_AT + RING_STEP}
+        stage_at = {(0, 0): FIRST_RAW_AT - 3072, (0, 4): FIRST_RAW_AT + 1024, (0, 5): LAST_RAW_AT + 1024, (1, 0): LEAD_STAGE_AT, (1, 3): RING_AT, (1, 4): RING_AT + RING_STEP}
         codes_at = {(1, e): RING_AT + RING_STEP * e for e in range(2)}
-        scale_at = {(0, 0): LAST_RAW_AT, (0, 4): LAST_RAW_AT + 512, (0, 5): LEAD_STAGE_AT}
+        scale_at = {(0, 0): LAST_RAW_AT, (0, 4): LEAD_STAGE_AT + 256, (0, 5): LEAD_STAGE_AT}
         for n, group in enumerate(groups):
             width = len(group) * C
             stage = place([P, width * PACK], BF16, "x_stage%d" % n, stage_at.get(group[0]))
@@ -296,8 +296,8 @@ def tile_moe_prv_lin_bias_kernel(tc, uT, wu, w_words, w_scales, b, gate, offs, o
         for e in range(4):
             project(0, e, 0)
         for rs in PAIRS:
-            round_wu(1, 0, LOW, rs, "vector")
-            round_wu(1, 0, HIGH, rs, "scalar")
+            round_wu(1, 0, slice(0, 40), rs, "vector")
+            round_wu(1, 0, slice(40, P), rs, "scalar")
         for rs in PAIRS:
             quantise_wu(1, 0, rs, slice(0, 2 * P))
         for e in range(4):
@@ -309,8 +309,8 @@ def tile_moe_prv_lin_bias_kernel(tc, uT, wu, w_words, w_scales, b, gate, offs, o
             for g in range(PASSES):
                 project(0, e, g)
         for rs in PAIRS:
-            round_wu(0, 1, slice(0, 72), rs, "vector")
-            round_wu(0, 1, slice(72, P), rs, "scalar")
+            round_wu(0, 1, slice(0, 64), rs, "vector")
+            round_wu(0, 1, slice(64, P), rs, "scalar")
         for rs in PAIRS:
             quantise_wu(0, 1, rs, slice(0, 2 * P))
         for e in range(E - 1):
@@ -325,13 +325,13 @@ def tile_moe_prv_lin_bias_kernel(tc, uT, wu, w_words, w_scales, b, gate, offs, o
                     quantise_wu(1, 1, rs, slice(r * P + ms.start, r * P + ms.stop))
         empty(0, 5)
         quantise_x(0, 3)
-        quantise_x(0, 4)
         for e in range(AHEAD):
             project(1, e, 1)
         for e in range(DEPTH):
             empty(1, e)
             quantise_x(1, e)
             if e == 0:
+                quantise_x(0, 4)
                 quantise_x(0, 5)
         for e in range(2):
             expert(e)

@@ -36,8 +36,8 @@ RING_AT, RING_STEP = 12288, 1024
 LEAD_STAGE_AT = 16384
 LAST_RAW_AT = 20480
 SECOND_RAW_AT = 24576
-THIRD_RAW_AT = 32768
-FIRST_RAW_AT = 45056
+OPENING_STAGE_AT = 32768
+FIRST_STAGE_AT = 45056
 
 
 def tile_moe_prv_lin_bias_kernel(tc, uT, wu, w_words, w_scales, b, gate, offs, out):
@@ -74,7 +74,7 @@ def tile_moe_prv_lin_bias_kernel(tc, uT, wu, w_words, w_scales, b, gate, offs, o
         wu_rows = wu.rearrange("(g p j) (a c) -> g a p j c", g=PASSES, p=P, a=PASSES)
         wu_raw = {}
         for g, a, ms in ((0, 0, slice(0, P)), (1, 0, slice(0, P)), (0, 1, slice(0, P)), (1, 1, LOW), (1, 1, HIGH)):
-            at = {(0, 0, 0): FIRST_RAW_AT, (1, 0, 0): SECOND_RAW_AT, (0, 1, 0): THIRD_RAW_AT, (1, 1, HIGH.start): LAST_RAW_AT}.get((g, a, ms.start))
+            at = {(1, 0, 0): SECOND_RAW_AT, (1, 1, HIGH.start): LAST_RAW_AT}.get((g, a, ms.start))
             tile = place([P, PACK, (ms.stop - ms.start) * PACK], F32, "wu_raw%d%d_%d" % (g, a, ms.start), at)
             nc.sync.dma_start(out=tile[:], in_=wu_rows[g, a][:, :, ms.start * PACK : ms.stop * PACK])
             wu_raw[g, a, ms.start] = tile
@@ -114,13 +114,13 @@ def tile_moe_prv_lin_bias_kernel(tc, uT, wu, w_words, w_scales, b, gate, offs, o
                 nc.gpsimd.memset(pairs[g, h][:, T:, :].rearrange("p t i -> p (t i)").bitcast(U32), 0)
         picked = [place([P, 2, S], U32, "picked%d" % g, PICKED_AT if g == 0 else None) for g in range(PASSES)]
         u_stage, u_codes, u_scale = {}, {}, {}
-        token_stage_at = {(0, EARLY.start): LAST_TOKENS_AT, (1, EARLY.start): PICKED_AT, (1, LATE.start): FIRST_RAW_AT}
+        token_stage_at = {(0, EARLY.start): LAST_TOKENS_AT, (1, EARLY.start): PICKED_AT, (1, LATE.start): FIRST_STAGE_AT}
         for g in range(PASSES):
             for cut in (EARLY, LATE):
                 width, key = cut.stop - cut.start, (g, cut.start)
                 u_stage[key] = place([P, width * PACK], BF16, "u_stage%d_%d" % key, token_stage_at.get(key))
                 u_codes[key] = place([P, width], U32, "u_codes%d_%d" % key)
-                u_scale[key] = place([P, width], U8, "u_scale%d_%d" % key, SECOND_RAW_AT + 2048 if key == (0, LATE.start) else None)
+                u_scale[key] = place([P, width], U8, "u_scale%d_%d" % key, {(0, LATE.start): SECOND_RAW_AT + 2048, (1, EARLY.start): OPENING_STAGE_AT}.get(key))
 
         def round_pairs(g, h, n, cut, engine):
             first = n * T // 2
@@ -168,7 +168,7 @@ def tile_moe_prv_lin_bias_kernel(tc, uT, wu, w_words, w_scales, b, gate, offs, o
             for g in range(PASSES):
                 for rs in parts(g, a):
                     key, count = (g, a, rs.start), rs.stop - rs.start
-                    wu_stage[key] = place([P, count * PASS], BF16, "wu_stage%d%d%d" % key)
+                    wu_stage[key] = place([P, count * PASS], BF16, "wu_stage%d%d%d" % key, {(0, 0, 0): OPENING_STAGE_AT, (0, 0, 2): FIRST_STAGE_AT, (0, 1, 0): SECOND_RAW_AT + 4096, (0, 1, 2): SECOND_RAW_AT + 6144}.get(key))
                     wu_codes[key] = place([P, count * P], U32, "wu_codes%d%d%d" % key)
                     wu_scale[key] = place([P, count * P], U8, "wu_scale%d%d%d" % key)
 
@@ -211,7 +211,7 @@ def tile_moe_prv_lin_bias_kernel(tc, uT, wu, w_words, w_scales, b, gate, offs, o
 
         x_stage, x_codes, x_scale, group_tiles = {}, {}, {}, {}
         groups = [[(0, e) for e in range(4)], [(0, 4)], [(0, 5)], [(1, 0)], [(1, 1)], [(1, 2)], [(1, 3)], [(1, 4), (1, 5)]]
-        stage_at = {(0, 0): FIRST_RAW_AT - 3072, (0, 4): FIRST_RAW_AT + 1024, (0, 5): LAST_RAW_AT + 1024, (1, 0): LEAD_STAGE_AT, (1, 3): RING_AT, (1, 4): RING_AT + RING_STEP}
+        stage_at = {(0, 0): FIRST_STAGE_AT - 3072, (0, 4): FIRST_STAGE_AT + 1024, (0, 5): LAST_RAW_AT + 1024, (1, 0): LEAD_STAGE_AT, (1, 3): RING_AT, (1, 4): RING_AT + RING_STEP}
         codes_at = {(1, e): RING_AT + RING_STEP * e for e in range(2)}
         scale_at = {(0, 0): LAST_RAW_AT, (0, 4): LEAD_STAGE_AT + 256, (0, 5): LEAD_STAGE_AT}
         for n, group in enumerate(groups):
@@ -288,16 +288,17 @@ def tile_moe_prv_lin_bias_kernel(tc, uT, wu, w_words, w_scales, b, gate, offs, o
             )
         interleave(1, EARLY, "vector")
         quantise_u(0, EARLY, slice(256, 512))
-        for rs in PAIRS:
-            round_wu(0, 0, slice(0, P), rs, "scalar")
-        quantise_u(1, EARLY, slice(0, 512))
+        round_wu(0, 0, HIGH, PAIRS[1], "gpsimd")
+        round_wu(0, 0, slice(0, P), PAIRS[0], "scalar")
+        round_wu(0, 0, LOW, PAIRS[1], "scalar")
         for rs in PAIRS:
             quantise_wu(0, 0, rs, slice(0, 2 * P))
+        quantise_u(1, EARLY, slice(0, 512))
         for e in range(4):
             project(0, e, 0)
         for rs in PAIRS:
-            round_wu(1, 0, slice(0, 40), rs, "vector")
-            round_wu(1, 0, slice(40, P), rs, "scalar")
+            round_wu(1, 0, slice(0, 32), rs, "vector")
+            round_wu(1, 0, slice(32, P), rs, "scalar")
         for rs in PAIRS:
             quantise_wu(1, 0, rs, slice(0, 2 * P))
         for e in range(4):
@@ -309,8 +310,8 @@ def tile_moe_prv_lin_bias_kernel(tc, uT, wu, w_words, w_scales, b, gate, offs, o
             for g in range(PASSES):
                 project(0, e, g)
         for rs in PAIRS:
-            round_wu(0, 1, slice(0, 64), rs, "vector")
-            round_wu(0, 1, slice(64, P), rs, "scalar")
+            round_wu(0, 1, slice(0, 48), rs, "vector")
+            round_wu(0, 1, slice(48, P), rs, "scalar")
         for rs in PAIRS:
             quantise_wu(0, 1, rs, slice(0, 2 * P))
         for e in range(E - 1):

@@ -13,6 +13,7 @@ U16 = mybir.dt.uint16
 U8 = mybir.dt.uint8
 FP8X4 = mybir.dt.float8_e4m3fn_x4
 IDENTITY = mybir.ActivationFunctionType.Identity
+COPY = mybir.ActivationFunctionType.Copy
 MULT = mybir.AluOpType.mult
 ADD = mybir.AluOpType.add
 
@@ -23,8 +24,7 @@ PASSES = 2
 S = E * C
 PER_COLUMN = 16
 WINDOW = 1024
-DEPTH = 3
-AHEAD = 5
+VECTOR_BANKS = ((0, 5), (1, 1), (1, 5))
 WARM_UP = 5
 EARLY, LATE = slice(0, 512), slice(512, S)
 EVERY = slice(0, 4)
@@ -32,7 +32,7 @@ PAIRS = (slice(0, 2), slice(2, 4))
 LOW, HIGH = slice(0, 64), slice(64, P)
 LAST_TOKENS_AT = 0
 PICKED_AT = 6144
-RING_AT, RING_STEP = 12288, 1024
+LEAD_CODES_AT = 12288
 LEAD_STAGE_AT = 16384
 LAST_RAW_AT = 20480
 SECOND_RAW_AT = 24576
@@ -57,7 +57,7 @@ def tile_moe_prv_lin_bias_kernel(tc, uT, wu, w_words, w_scales, b, gate, offs, o
             return banks[((0, 1, 2, 3, 4, 5), (6, 7, 0, 1, 2, 3))[a][e]]
 
         def sum_bank(e):
-            return banks[(e + 3) % 8]
+            return banks[(4, 6, 7, 0, 1, 2)[e]]
 
         def columns(e):
             return slice(e * C, (e + 1) * C)
@@ -89,7 +89,7 @@ def tile_moe_prv_lin_bias_kernel(tc, uT, wu, w_words, w_scales, b, gate, offs, o
             for e in range(first, first + count):
                 gate_tiles[e] = (tile, first)
 
-        load_gate(0, 2)
+        load_gate(0, 3)
         w_scale = place([P, E * PASSES, N], U8, "w_scale")
         nc.gpsimd.memset(w_scale[:].bitcast(I32), 0)
         scale_src = w_scales.rearrange("e a q n -> q (e a) n")
@@ -105,7 +105,7 @@ def tile_moe_prv_lin_bias_kernel(tc, uT, wu, w_words, w_scales, b, gate, offs, o
             nc.sync.dma_start(out=tile[:].bitcast(I32), in_=w_src[:, first * PASSES : (first + 2) * PASSES].bitcast(I32))
             for n in range(2 * PASSES):
                 w_codes[first + n // PASSES, n % PASSES] = tile[:, n, :]
-        load_gate(2, E - 2)
+        load_gate(3, E - 3)
 
         pairs = {}
         for g in range(PASSES):
@@ -118,7 +118,8 @@ def tile_moe_prv_lin_bias_kernel(tc, uT, wu, w_words, w_scales, b, gate, offs, o
         for g in range(PASSES):
             for cut in (EARLY, LATE):
                 width, key = cut.stop - cut.start, (g, cut.start)
-                u_stage[key] = place([P, width * PACK], BF16, "u_stage%d_%d" % key, token_stage_at.get(key))
+                room = 4096 if key == (1, LATE.start) else width * PACK
+                u_stage[key] = place([P, room], BF16, "u_stage%d_%d" % key, token_stage_at.get(key))[:, : width * PACK]
                 u_codes[key] = place([P, width], U32, "u_codes%d_%d" % key)
                 u_scale[key] = place([P, width], U8, "u_scale%d_%d" % key, {(0, LATE.start): SECOND_RAW_AT + 2048, (1, EARLY.start): OPENING_STAGE_AT}.get(key))
 
@@ -140,7 +141,7 @@ def tile_moe_prv_lin_bias_kernel(tc, uT, wu, w_words, w_scales, b, gate, offs, o
             nc.vector.tensor_copy(out=picked[g][:, h, :], in_=window.indirect(offsets[:]))
 
         def interleave(g, cut, engine):
-            stage = u_stage[g, cut.start][:]
+            stage = u_stage[g, cut.start]
             if engine == "vector":
                 nc.vector.tensor_copy(
                     out=stage.rearrange("p (s h i) -> p s h i", h=2, i=2),
@@ -210,14 +211,18 @@ def tile_moe_prv_lin_bias_kernel(tc, uT, wu, w_words, w_scales, b, gate, offs, o
                 )
 
         x_stage, x_codes, x_scale, group_tiles = {}, {}, {}, {}
-        groups = [[(0, e) for e in range(4)], [(0, 4)], [(0, 5)], [(1, 0)], [(1, 1)], [(1, 2)], [(1, 3)], [(1, 4), (1, 5)]]
-        stage_at = {(0, 0): FIRST_STAGE_AT - 3072, (0, 4): FIRST_STAGE_AT + 1024, (0, 5): LAST_RAW_AT + 1024, (1, 0): LEAD_STAGE_AT, (1, 3): RING_AT, (1, 4): RING_AT + RING_STEP}
-        codes_at = {(1, e): RING_AT + RING_STEP * e for e in range(2)}
-        scale_at = {(0, 0): LAST_RAW_AT, (0, 4): LEAD_STAGE_AT + 256, (0, 5): LEAD_STAGE_AT}
+        groups = [[(0, e) for e in range(4)], [(1, 0)], [(1, 1)], [(1, 2)], [(1, 3)], [(0, 4), (1, 4)], [(0, 5)], [(1, 5)]]
+        stage_at = {(0, 0): FIRST_STAGE_AT, (0, 4): FIRST_STAGE_AT + 4096, (1, 0): LEAD_STAGE_AT, (0, 5): LEAD_STAGE_AT, (1, 5): LEAD_CODES_AT + 2048}
+        scale_at = {(0, 0): LAST_RAW_AT}
+        for n, key in enumerate(((1, 2), (1, 3), (0, 4), (0, 5))):
+            scale_at[key] = LEAD_CODES_AT + 256 * n
         for n, group in enumerate(groups):
             width = len(group) * C
             stage = place([P, width * PACK], BF16, "x_stage%d" % n, stage_at.get(group[0]))
-            codes = place([P, width], U32, "x_codes%d" % n, codes_at.get(group[0]))
+            if group[0] == (1, 0):
+                codes = place([P, 8 * width], U32, "x_codes%d" % n, LEAD_CODES_AT)[:, :width]
+            else:
+                codes = place([P, width], U32, "x_codes%d" % n)
             scale = place([P, width], U8, "x_scale%d" % n, scale_at.get(group[0]))
             group_tiles[group[-1]] = (stage, codes, scale)
             for i, key in enumerate(group):
@@ -228,7 +233,7 @@ def tile_moe_prv_lin_bias_kernel(tc, uT, wu, w_words, w_scales, b, gate, offs, o
         def empty(a, e):
             dst = x_stage[a, e].rearrange("p (s r) -> p s r", r=PACK)
             src = bank_of(a, e)[:].rearrange("p r s -> p s r")
-            if (a, e) == (0, E - 1):
+            if (a, e) in VECTOR_BANKS:
                 nc.vector.tensor_copy(out=dst, in_=src)
             else:
                 nc.scalar.copy(out=dst, in_=src)
@@ -237,9 +242,11 @@ def tile_moe_prv_lin_bias_kernel(tc, uT, wu, w_words, w_scales, b, gate, offs, o
             stage, codes, scale = group_tiles[a, e]
             nc.vector.quantize_mx(out=codes[:].bitcast(FP8X4), scales=scale[:], in_=stage[:])
 
-        sum_tiles = {e: place([P, count * C], F32, "sums%d" % e) for e, count in ((0, 1), (1, 1), (2, 2), (4, 2))}
-        sums = [sum_tiles[0], sum_tiles[1], sum_tiles[2][:, :C], sum_tiles[2][:, C:], sum_tiles[4][:, :C], sum_tiles[4][:, C:]]
-        result = place([P, T], F32, "result")
+        gated = [place([P, 2 * C], F32, "gated%d" % n) for n in range(E // 2)]
+        windows = {engine: place([P, T], F32, "window_" + engine) for engine in ("scalar", "vector")}
+        for window in windows.values():
+            nc.vector.memset(window[:], 0.0)
+        result = [place([P, T // 2], F32, "result%d" % n) for n in range(2)]
 
         def expert(e):
             for a in range(PASSES):
@@ -253,13 +260,18 @@ def tile_moe_prv_lin_bias_kernel(tc, uT, wu, w_words, w_scales, b, gate, offs, o
                     stop=(a == PASSES - 1),
                 )
 
-        def add_bias(e):
-            nc.scalar.activation(sums[e][:], sum_bank(e)[:, 0, :], IDENTITY, bias=bias[:, e : e + 1])
-
-        def scatter(e, count):
-            slots = offsets[:, e * C // PER_COLUMN : (e + count) * C // PER_COLUMN]
+        def bias_and_gate(e):
             tile, first = gate_tiles[e]
-            nc.vector.tensor_tensor(result[:].indirect(slots), sum_tiles[e][:], tile[:, (e - first) * C : (e - first + count) * C], MULT)
+            nc.vector.scalar_tensor_tensor(
+                gated[e // 2][:, columns(e % 2)], sum_bank(e)[:, 0, :], bias[:, e : e + 1], tile[:, (e - first) * C : (e - first + 1) * C], ADD, MULT
+            )
+
+        def scatter(n, engine):
+            slots = offsets[:, 2 * n * C // PER_COLUMN : 2 * (n + 1) * C // PER_COLUMN]
+            if engine == "vector":
+                nc.vector.tensor_copy(out=windows[engine][:].indirect(slots), in_=gated[n][:])
+            else:
+                nc.scalar.activation(windows[engine][:].indirect(slots), gated[n][:], COPY)
 
         round_pairs(0, 0, 0, slice(0, 528), "vector")
         round_pairs(0, 0, 0, slice(528, T), "scalar")
@@ -316,7 +328,7 @@ def tile_moe_prv_lin_bias_kernel(tc, uT, wu, w_words, w_scales, b, gate, offs, o
             quantise_wu(0, 1, rs, slice(0, 2 * P))
         for e in range(E - 1):
             empty(0, e)
-        for e in range(AHEAD):
+        for e in range(E):
             project(1, e, 0)
         for ms in (LOW, HIGH):
             for rs in PAIRS:
@@ -324,31 +336,32 @@ def tile_moe_prv_lin_bias_kernel(tc, uT, wu, w_words, w_scales, b, gate, offs, o
             for rs in PAIRS:
                 for r in range(2):
                     quantise_wu(1, 1, rs, slice(r * P + ms.start, r * P + ms.stop))
-        empty(0, 5)
         quantise_x(0, 3)
-        for e in range(AHEAD):
+        for e in range(E):
             project(1, e, 1)
-        for e in range(DEPTH):
+        for e in range(E - 1):
             empty(1, e)
+        for e in range(2):
             quantise_x(1, e)
-            if e == 0:
-                quantise_x(0, 4)
-                quantise_x(0, 5)
+        empty(0, E - 1)
         for e in range(2):
             expert(e)
-            add_bias(e)
-            scatter(e, 1)
-            if e == 0:
-                for g in range(PASSES):
-                    project(1, E - 1, g)
-                empty(1, 3)
-                quantise_x(1, 3)
-        empty(1, 4)
-        empty(1, 5)
-        quantise_x(1, 5)
-        for e in range(2, E):
+            bias_and_gate(e)
+        scatter(0, "scalar")
+        for e in range(2, 4):
+            quantise_x(1, e)
             expert(e)
-            add_bias(e)
-            if e % 2:
-                scatter(e - 1, 2)
-        nc.sync.dma_start(out=out, in_=result[:])
+        empty(1, E - 1)
+        quantise_x(1, 4)
+        expert(4)
+        quantise_x(0, 5)
+        quantise_x(1, 5)
+        expert(5)
+        for e in range(2, E):
+            bias_and_gate(e)
+        scatter(2, "scalar")
+        scatter(1, "vector")
+        for n in range(2):
+            half = slice(n * T // 2, (n + 1) * T // 2)
+            nc.vector.tensor_tensor(result[n][:], windows["scalar"][:, half], windows["vector"][:, half], ADD)
+            nc.sync.dma_start(out=out[:, half], in_=result[n][:])

@@ -24,7 +24,9 @@ PASSES = 2
 S = E * C
 PER_COLUMN = 16
 WINDOW = 1024
-VECTOR_BANKS = ((0, 5), (1, 1), (1, 5))
+AHEAD = 5
+VECTOR_BANKS = ((1, 0), (1, 5))
+SCATTERS = (("scalar", 0, 256), ("vector", 256, 544), ("scalar", 544, 768))
 WARM_UP = 5
 EARLY, LATE = slice(0, 512), slice(512, S)
 EVERY = slice(0, 4)
@@ -32,8 +34,6 @@ PAIRS = (slice(0, 2), slice(2, 4))
 LOW, HIGH = slice(0, 64), slice(64, P)
 LAST_TOKENS_AT = 0
 PICKED_AT = 6144
-LEAD_CODES_AT = 12288
-LEAD_STAGE_AT = 16384
 LAST_RAW_AT = 20480
 SECOND_RAW_AT = 24576
 OPENING_STAGE_AT = 32768
@@ -54,10 +54,10 @@ def tile_moe_prv_lin_bias_kernel(tc, uT, wu, w_words, w_scales, b, gate, offs, o
             return shared.tile(shape, dtype, name=name, offset=at, align_bytes=256)
 
         def bank_of(a, e):
-            return banks[((0, 1, 2, 3, 4, 5), (6, 7, 0, 1, 2, 3))[a][e]]
+            return banks[((0, 1, 2, 3, 4, 5), (6, 7, 0, 1, 2, 5))[a][e]]
 
         def sum_bank(e):
-            return banks[(4, 6, 7, 0, 1, 2)[e]]
+            return banks[(3, 4, 6, 7, 0, 1)[e]]
 
         def columns(e):
             return slice(e * C, (e + 1) * C)
@@ -71,41 +71,38 @@ def tile_moe_prv_lin_bias_kernel(tc, uT, wu, w_words, w_scales, b, gate, offs, o
             nc.sync.dma_start(out=u_raw[g, h, 0][:], in_=u_rows[g, h])
             if (g, h) == (0, 0):
                 nc.sync.dma_start(offsets[:], offs)
+        bias = place([P, E], F32, "bias")
+        w_scale = place([P, E * PASSES, N], U8, "w_scale")
+        nc.gpsimd.memset(w_scale[:].bitcast(I32), 0)
+        scale_src = w_scales.rearrange("e a q n -> q (e a) n")
         wu_rows = wu.rearrange("(g p j) (a c) -> g a p j c", g=PASSES, p=P, a=PASSES)
         wu_raw = {}
         for g, a, ms in ((0, 0, slice(0, P)), (1, 0, slice(0, P)), (0, 1, slice(0, P)), (1, 1, LOW), (1, 1, HIGH)):
+            if ms == LOW:
+                nc.sync.dma_start(out=bias[:], in_=b)
+                for quad in range(4):
+                    nc.sync.dma_start(
+                        out=w_scale[32 * quad : 32 * quad + 4, :, :].bitcast(I32),
+                        in_=scale_src[4 * quad : 4 * quad + 4].bitcast(I32),
+                    )
             at = {(1, 0, 0): SECOND_RAW_AT, (1, 1, HIGH.start): LAST_RAW_AT}.get((g, a, ms.start))
             tile = place([P, PACK, (ms.stop - ms.start) * PACK], F32, "wu_raw%d%d_%d" % (g, a, ms.start), at)
             nc.sync.dma_start(out=tile[:], in_=wu_rows[g, a][:, :, ms.start * PACK : ms.stop * PACK])
             wu_raw[g, a, ms.start] = tile
 
-        bias = place([P, E], F32, "bias")
-        nc.sync.dma_start(out=bias[:], in_=b)
-        gate_tiles = {}
-
-        def load_gate(first, count):
-            tile = place([P, count * C], F32, "gate%d" % first)
-            nc.sync.dma_start(out=tile[:], in_=gate[:, first * C : (first + count) * C])
-            for e in range(first, first + count):
-                gate_tiles[e] = (tile, first)
-
-        load_gate(0, 3)
-        w_scale = place([P, E * PASSES, N], U8, "w_scale")
-        nc.gpsimd.memset(w_scale[:].bitcast(I32), 0)
-        scale_src = w_scales.rearrange("e a q n -> q (e a) n")
-        for quad in range(4):
-            nc.sync.dma_start(
-                out=w_scale[32 * quad : 32 * quad + 4, :, :].bitcast(I32),
-                in_=scale_src[4 * quad : 4 * quad + 4].bitcast(I32),
-            )
         w_src = w_words.rearrange("e a p n r -> p (e a) (n r)")
-        w_codes = {}
+        w_codes, gate_tiles = {}, {}
         for first in range(0, E, 2):
             tile = place([P, 2 * PASSES, N * PACK], U8, "w_codes%d" % first)
             nc.sync.dma_start(out=tile[:].bitcast(I32), in_=w_src[:, first * PASSES : (first + 2) * PASSES].bitcast(I32))
             for n in range(2 * PASSES):
                 w_codes[first + n // PASSES, n % PASSES] = tile[:, n, :]
-        load_gate(3, E - 3)
+            if first < 4:
+                start, count = ((0, 2), (2, 4))[first // 2]
+                tile = place([P, count * C], F32, "gate%d" % start)
+                nc.sync.dma_start(out=tile[:], in_=gate[:, start * C : (start + count) * C])
+                for e in range(start, start + count):
+                    gate_tiles[e] = (tile, start)
 
         pairs = {}
         for g in range(PASSES):
@@ -211,18 +208,13 @@ def tile_moe_prv_lin_bias_kernel(tc, uT, wu, w_words, w_scales, b, gate, offs, o
                 )
 
         x_stage, x_codes, x_scale, group_tiles = {}, {}, {}, {}
-        groups = [[(0, e) for e in range(4)], [(1, 0)], [(1, 1)], [(1, 2)], [(1, 3)], [(0, 4), (1, 4)], [(0, 5)], [(1, 5)]]
-        stage_at = {(0, 0): FIRST_STAGE_AT, (0, 4): FIRST_STAGE_AT + 4096, (1, 0): LEAD_STAGE_AT, (0, 5): LEAD_STAGE_AT, (1, 5): LEAD_CODES_AT + 2048}
-        scale_at = {(0, 0): LAST_RAW_AT}
-        for n, key in enumerate(((1, 2), (1, 3), (0, 4), (0, 5))):
-            scale_at[key] = LEAD_CODES_AT + 256 * n
+        groups = [[(0, e) for e in range(4)], [(0, 4)], [(0, 5)]] + [[(1, e)] for e in range(E)]
+        stage_at = {(0, 0): FIRST_STAGE_AT, (0, 4): FIRST_STAGE_AT + 4096, (0, 5): LAST_RAW_AT + 1024}
+        scale_at = {(0, 0): LAST_RAW_AT, (0, 4): LAST_RAW_AT + 512}
         for n, group in enumerate(groups):
             width = len(group) * C
             stage = place([P, width * PACK], BF16, "x_stage%d" % n, stage_at.get(group[0]))
-            if group[0] == (1, 0):
-                codes = place([P, 8 * width], U32, "x_codes%d" % n, LEAD_CODES_AT)[:, :width]
-            else:
-                codes = place([P, width], U32, "x_codes%d" % n)
+            codes = place([P, width], U32, "x_codes%d" % n)
             scale = place([P, width], U8, "x_scale%d" % n, scale_at.get(group[0]))
             group_tiles[group[-1]] = (stage, codes, scale)
             for i, key in enumerate(group):
@@ -242,7 +234,7 @@ def tile_moe_prv_lin_bias_kernel(tc, uT, wu, w_words, w_scales, b, gate, offs, o
             stage, codes, scale = group_tiles[a, e]
             nc.vector.quantize_mx(out=codes[:].bitcast(FP8X4), scales=scale[:], in_=stage[:])
 
-        gated = [place([P, 2 * C], F32, "gated%d" % n) for n in range(E // 2)]
+        gated = place([P, S], F32, "gated")
         windows = {engine: place([P, T], F32, "window_" + engine) for engine in ("scalar", "vector")}
         for window in windows.values():
             nc.vector.memset(window[:], 0.0)
@@ -263,15 +255,15 @@ def tile_moe_prv_lin_bias_kernel(tc, uT, wu, w_words, w_scales, b, gate, offs, o
         def bias_and_gate(e):
             tile, first = gate_tiles[e]
             nc.vector.scalar_tensor_tensor(
-                gated[e // 2][:, columns(e % 2)], sum_bank(e)[:, 0, :], bias[:, e : e + 1], tile[:, (e - first) * C : (e - first + 1) * C], ADD, MULT
+                gated[:, columns(e)], sum_bank(e)[:, 0, :], bias[:, e : e + 1], tile[:, (e - first) * C : (e - first + 1) * C], ADD, MULT
             )
 
-        def scatter(n, engine):
-            slots = offsets[:, 2 * n * C // PER_COLUMN : 2 * (n + 1) * C // PER_COLUMN]
+        def scatter(engine, first, last):
+            slots = offsets[:, first // PER_COLUMN : last // PER_COLUMN]
             if engine == "vector":
-                nc.vector.tensor_copy(out=windows[engine][:].indirect(slots), in_=gated[n][:])
+                nc.vector.tensor_copy(out=windows[engine][:].indirect(slots), in_=gated[:, first:last])
             else:
-                nc.scalar.activation(windows[engine][:].indirect(slots), gated[n][:], COPY)
+                nc.scalar.activation(windows[engine][:].indirect(slots), gated[:, first:last], COPY)
 
         round_pairs(0, 0, 0, slice(0, 528), "vector")
         round_pairs(0, 0, 0, slice(528, T), "scalar")
@@ -328,7 +320,7 @@ def tile_moe_prv_lin_bias_kernel(tc, uT, wu, w_words, w_scales, b, gate, offs, o
             quantise_wu(0, 1, rs, slice(0, 2 * P))
         for e in range(E - 1):
             empty(0, e)
-        for e in range(E):
+        for e in range(AHEAD):
             project(1, e, 0)
         for ms in (LOW, HIGH):
             for rs in PAIRS:
@@ -337,30 +329,29 @@ def tile_moe_prv_lin_bias_kernel(tc, uT, wu, w_words, w_scales, b, gate, offs, o
                 for r in range(2):
                     quantise_wu(1, 1, rs, slice(r * P + ms.start, r * P + ms.stop))
         quantise_x(0, 3)
-        for e in range(E):
-            project(1, e, 1)
-        for e in range(E - 1):
-            empty(1, e)
-        for e in range(2):
-            quantise_x(1, e)
         empty(0, E - 1)
+        for e in range(AHEAD):
+            project(1, e, 1)
+            empty(1, e)
+        quantise_x(0, 4)
         for e in range(2):
-            expert(e)
-            bias_and_gate(e)
-        scatter(0, "scalar")
-        for e in range(2, 4):
             quantise_x(1, e)
             expert(e)
-        empty(1, E - 1)
-        quantise_x(1, 4)
-        expert(4)
+        for g in range(PASSES):
+            project(1, E - 1, g)
         quantise_x(0, 5)
-        quantise_x(1, 5)
-        expert(5)
+        for e in range(2):
+            bias_and_gate(e)
+        scatter(*SCATTERS[0])
+        for e in range(2, E):
+            if e == E - 2:
+                empty(1, E - 1)
+            quantise_x(1, e)
+            expert(e)
         for e in range(2, E):
             bias_and_gate(e)
-        scatter(2, "scalar")
-        scatter(1, "vector")
+        scatter(*SCATTERS[2])
+        scatter(*SCATTERS[1])
         for n in range(2):
             half = slice(n * T // 2, (n + 1) * T // 2)
             nc.vector.tensor_tensor(result[n][:], windows["scalar"][:, half], windows["vector"][:, half], ADD)

@@ -24,7 +24,7 @@ PASSES = 2
 S = E * C
 PER_COLUMN = 16
 WINDOW = 1024
-AHEAD = 5
+AHEAD = 4
 VECTOR_BANKS = ((1, 0), (1, 5))
 SCATTERS = (("scalar", 0, 256), ("vector", 256, 544), ("scalar", 544, 768))
 WARM_UP = 5
@@ -54,10 +54,10 @@ def tile_moe_prv_lin_bias_kernel(tc, uT, wu, w_words, w_scales, b, gate, offs, o
             return shared.tile(shape, dtype, name=name, offset=at, align_bytes=256)
 
         def bank_of(a, e):
-            return banks[((0, 1, 2, 3, 4, 5), (6, 7, 0, 1, 2, 5))[a][e]]
+            return banks[((0, 1, 2, 3, 4, 5), (6, 7, 0, 1, 5, 7))[a][e]]
 
         def sum_bank(e):
-            return banks[(3, 4, 6, 7, 0, 1)[e]]
+            return banks[(2, 3, 4, 6, 0, 1)[e]]
 
         def columns(e):
             return slice(e * C, (e + 1) * C)
@@ -330,7 +330,9 @@ def tile_moe_prv_lin_bias_kernel(tc, uT, wu, w_words, w_scales, b, gate, offs, o
                     quantise_wu(1, 1, rs, slice(r * P + ms.start, r * P + ms.stop))
         quantise_x(0, 3)
         empty(0, E - 1)
-        for e in range(AHEAD):
+        for e in range(E - 1):
+            if e >= AHEAD:
+                project(1, e, 0)
             project(1, e, 1)
             empty(1, e)
         quantise_x(0, 4)

from contextlib import ExitStack

import concourse.mybir as mybir

M, K, T, E, C, N = 1024, 1024, 768, 6, 128, 128
FLOPS = 2 * M * K * T + 2 * K * N * E * C

F32 = mybir.dt.float32
BF16 = mybir.dt.bfloat16
I32 = mybir.dt.int32
U32 = mybir.dt.uint32
U16 = mybir.dt.uint16
U8 = mybir.dt.uint8
FP8X4 = mybir.dt.float8_e4m3fn_x4
IDENTITY = mybir.ActivationFunctionType.Identity
COPY = mybir.ActivationFunctionType.Copy
MULT = mybir.AluOpType.mult
ADD = mybir.AluOpType.add

P = 128
PACK = 4
PASS = P * PACK
PASSES = 2
S = E * C
PER_COLUMN = 16
WINDOW = 1024
AHEAD = 4
VECTOR_BANKS = ((1, 0), (1, 5))
SCATTERS = (("scalar", 0, 256), ("vector", 256, 544), ("scalar", 544, 768))
WARM_UP = 5
EARLY, LATE = slice(0, 512), slice(512, S)
EVERY = slice(0, 4)
PAIRS = (slice(0, 2), slice(2, 4))
LOW, HIGH = slice(0, 64), slice(64, P)
LAST_TOKENS_AT = 0
PICKED_AT = 6144
LAST_RAW_AT = 20480
SECOND_RAW_AT = 24576
OPENING_STAGE_AT = 32768
FIRST_STAGE_AT = 45056


def tile_moe_prv_lin_bias_kernel(tc, uT, wu, w_words, w_scales, b, gate, offs, out):
    nc = tc.nc
    with ExitStack() as ctx:
        keep = ctx.enter_context(tc.tile_pool(name="keep", bufs=1))
        shared = ctx.enter_context(tc.tile_pool(name="shared", bufs=1))
        psum = ctx.enter_context(tc.psum_pool(name="psum", bufs=1))
        banks = [psum.tile([P, PACK, C], F32, name="bank%d" % i) for i in range(8)]

        def place(shape, dtype, name, at=None):
            if at is None:
                return keep.tile(shape, dtype, name=name, align_bytes=256)
            return shared.tile(shape, dtype, name=name, offset=at, align_bytes=256)

        def bank_of(a, e):
            return banks[((0, 1, 2, 3, 4, 5), (6, 7, 0, 1, 5, 7))[a][e]]

        def sum_bank(e):
            return banks[(2, 3, 4, 6, 0, 1)[e]]

        def columns(e):
            return slice(e * C, (e + 1) * C)

        offsets = keep.tile([P, S // PER_COLUMN], U16, name="offsets")

        u_rows = uT.rearrange("(g p h i) t -> g h p i t", g=PASSES, p=P, h=2)
        u_raw = {}
        for g, h in ((0, 0), (0, 1), (1, 0), (1, 1)):
            u_raw[g, h, 0] = place([P, 2, T], F32, "u_raw%d%d" % (g, h), LAST_TOKENS_AT if (g, h) == (1, 1) else None)
            nc.sync.dma_start(out=u_raw[g, h, 0][:], in_=u_rows[g, h])
            if (g, h) == (0, 0):
                nc.sync.dma_start(offsets[:], offs)
        bias = place([P, E], F32, "bias")
        w_scale = place([P, E * PASSES, N], U8, "w_scale")
        nc.gpsimd.memset(w_scale[:].bitcast(I32), 0)
        scale_src = w_scales.rearrange("e a q n -> q (e a) n")
        wu_rows = wu.rearrange("(g p j) (a c) -> g a p j c", g=PASSES, p=P, a=PASSES)
        wu_raw = {}
        for g, a, ms in ((0, 0, slice(0, P)), (1, 0, slice(0, P)), (0, 1, slice(0, P)), (1, 1, LOW), (1, 1, HIGH)):
            if ms == LOW:
                nc.sync.dma_start(out=bias[:], in_=b)
                for quad in range(4):
                    nc.sync.dma_start(
                        out=w_scale[32 * quad : 32 * quad + 4, :, :].bitcast(I32),
                        in_=scale_src[4 * quad : 4 * quad + 4].bitcast(I32),
                    )
            at = {(1, 0, 0): SECOND_RAW_AT, (1, 1, HIGH.start): LAST_RAW_AT}.get((g, a, ms.start))
            tile = place([P, PACK, (ms.stop - ms.start) * PACK], F32, "wu_raw%d%d_%d" % (g, a, ms.start), at)
            nc.sync.dma_start(out=tile[:], in_=wu_rows[g, a][:, :, ms.start * PACK : ms.stop * PACK])
            wu_raw[g, a, ms.start] = tile

        w_src = w_words.rearrange("e a p n r -> p (e a) (n r)")
        w_codes, gate_tiles = {}, {}
        for first in range(0, E, 2):
            tile = place([P, 2 * PASSES, N * PACK], U8, "w_codes%d" % first)
            nc.sync.dma_start(out=tile[:].bitcast(I32), in_=w_src[:, first * PASSES : (first + 2) * PASSES].bitcast(I32))
            for n in range(2 * PASSES):
                w_codes[first + n // PASSES, n % PASSES] = tile[:, n, :]
            if first < 4:
                start, count = ((0, 2), (2, 4))[first // 2]
                tile = place([P, count * C], F32, "gate%d" % start)
                nc.sync.dma_start(out=tile[:], in_=gate[:, start * C : (start + count) * C])
                for e in range(start, start + count):
                    gate_tiles[e] = (tile, start)

        pairs = {}
        for g in range(PASSES):
            for h in range(2):
                pairs[g, h] = place([P, WINDOW, 2], BF16, "pairs%d%d" % (g, h))
                nc.gpsimd.memset(pairs[g, h][:, T:, :].rearrange("p t i -> p (t i)").bitcast(U32), 0)
        picked = [place([P, 2, S], U32, "picked%d" % g, PICKED_AT if g == 0 else None) for g in range(PASSES)]
        u_stage, u_codes, u_scale = {}, {}, {}
        token_stage_at = {(0, EARLY.start): LAST_TOKENS_AT, (1, EARLY.start): PICKED_AT, (1, LATE.start): FIRST_STAGE_AT}
        for g in range(PASSES):
            for cut in (EARLY, LATE):
                width, key = cut.stop - cut.start, (g, cut.start)
                room = 4096 if key == (1, LATE.start) else width * PACK
                u_stage[key] = place([P, room], BF16, "u_stage%d_%d" % key, token_stage_at.get(key))[:, : width * PACK]
                u_codes[key] = place([P, width], U32, "u_codes%d_%d" % key)
                u_scale[key] = place([P, width], U8, "u_scale%d_%d" % key, {(0, LATE.start): SECOND_RAW_AT + 2048, (1, EARLY.start): OPENING_STAGE_AT}.get(key))

        def round_pairs(g, h, n, cut, engine):
            first = n * T // 2
            dst = pairs[g, h][:, first + cut.start : first + cut.stop, :]
            src = u_raw[g, h, n][:, :, cut].rearrange("p i t -> p t i")
            if engine == "vector":
                nc.vector.tensor_copy(out=dst, in_=src)
            elif engine == "gpsimd":
                nc.gpsimd.tensor_scalar(dst, src, 1.0, 0.0, MULT, ADD)
            elif (g, h) == (0, 0):
                nc.scalar.activation(dst, src, IDENTITY)
            else:
                nc.scalar.copy(out=dst, in_=src)

        def gather(g, h):
            window = pairs[g, h][:].rearrange("p t i -> p (t i)").bitcast(U32)
            nc.vector.tensor_copy(out=picked[g][:, h, :], in_=window.indirect(offsets[:]))

        def interleave(g, cut, engine):
            stage = u_stage[g, cut.start]
            if engine == "vector":
                nc.vector.tensor_copy(
                    out=stage.rearrange("p (s h i) -> p s h i", h=2, i=2),
                    in_=picked[g][:].bitcast(BF16).rearrange("p h (s i) -> p s h i", i=2)[:, cut],
                )
            else:
                nc.scalar.copy(
                    out=stage.bitcast(U32).rearrange("p (s h) -> p s h", h=2),
                    in_=picked[g][:].rearrange("p h s -> p s h")[:, cut],
                )

        def quantise_u(g, cut, words):
            key = (g, cut.start)
            nc.vector.quantize_mx(
                out=u_codes[key][:, words].bitcast(FP8X4),
                scales=u_scale[key][:, words],
                in_=u_stage[key][:, words.start * PACK : words.stop * PACK],
            )

        def parts(g, a):
            return PAIRS

        wu_stage, wu_codes, wu_scale = {}, {}, {}
        for a in range(PASSES):
            for g in range(PASSES):
                for rs in parts(g, a):
                    key, count = (g, a, rs.start), rs.stop - rs.start
                    wu_stage[key] = place([P, count * PASS], BF16, "wu_stage%d%d%d" % key, {(0, 0, 0): OPENING_STAGE_AT, (0, 0, 2): FIRST_STAGE_AT, (0, 1, 0): SECOND_RAW_AT + 4096, (0, 1, 2): SECOND_RAW_AT + 6144}.get(key))
                    wu_codes[key] = place([P, count * P], U32, "wu_codes%d%d%d" % key)
                    wu_scale[key] = place([P, count * P], U8, "wu_scale%d%d%d" % key)

        def round_wu(g, a, ms, rs, engine):
            first = max(key[2] for key in wu_raw if key[:2] == (g, a) and key[2] <= ms.start)
            dst = wu_stage[g, a, rs.start][:].rearrange("p (r m j) -> p m j r", m=P, j=PACK)[:, ms]
            src = wu_raw[g, a, first][:].rearrange("p j (m r) -> p m j r", r=PACK)[:, ms.start - first : ms.stop - first, :, rs]
            if engine == "vector":
                nc.vector.tensor_copy(out=dst, in_=src)
            elif engine == "gpsimd":
                walk = "p m j r -> p m r j"
                nc.gpsimd.tensor_scalar(dst.rearrange(walk), src.rearrange(walk), 1.0, 0.0, MULT, ADD)
            else:
                nc.scalar.copy(out=dst, in_=src)

        def quantise_wu(g, a, rs, words):
            key = (g, a, rs.start)
            nc.vector.quantize_mx(
                out=wu_codes[key][:, words].bitcast(FP8X4),
                scales=wu_scale[key][:, words],
                in_=wu_stage[key][:, words.start * PACK : words.stop * PACK],
            )

        def project(a, e, g):
            cut = EARLY if e * C < LATE.start else LATE
            slots = slice(e * C - cut.start, (e + 1) * C - cut.start)
            order = (0, 1, 2, 3)
            for r in order:
                first = max(rs.start for rs in parts(g, a) if rs.start <= r)
                words = slice((r - first) * P, (r - first + 1) * P)
                nc.tensor.matmul_mx(
                    out=bank_of(a, e)[:, r, :],
                    lhsT=wu_codes[g, a, first][:, words].bitcast(FP8X4),
                    lhsT_scale=wu_scale[g, a, first][:, words],
                    rhs=u_codes[g, cut.start][:, slots].bitcast(FP8X4),
                    rhs_scale=u_scale[g, cut.start][:, slots],
                    start=(g == 0 and r == order[0]),
                    stop=(g == PASSES - 1 and r == PACK - 1),
                )

        x_stage, x_codes, x_scale, group_tiles = {}, {}, {}, {}
        groups = [[(0, e) for e in range(4)], [(0, 4)], [(0, 5)]] + [[(1, e)] for e in range(E)]
        stage_at = {(0, 0): FIRST_STAGE_AT, (0, 4): FIRST_STAGE_AT + 4096, (0, 5): LAST_RAW_AT + 1024}
        scale_at = {(0, 0): LAST_RAW_AT, (0, 4): LAST_RAW_AT + 512}
        for n, group in enumerate(groups):
            width = len(group) * C
            stage = place([P, width * PACK], BF16, "x_stage%d" % n, stage_at.get(group[0]))
            codes = place([P, width], U32, "x_codes%d" % n)
            scale = place([P, width], U8, "x_scale%d" % n, scale_at.get(group[0]))
            group_tiles[group[-1]] = (stage, codes, scale)
            for i, key in enumerate(group):
                x_stage[key] = stage[:, i * C * PACK : (i + 1) * C * PACK]
                x_codes[key] = codes[:, i * C : (i + 1) * C]
                x_scale[key] = scale[:, i * C : (i + 1) * C]

        def empty(a, e):
            dst = x_stage[a, e].rearrange("p (s r) -> p s r", r=PACK)
            src = bank_of(a, e)[:].rearrange("p r s -> p s r")
            if (a, e) in VECTOR_BANKS:
                nc.vector.tensor_copy(out=dst, in_=src)
            else:
                nc.scalar.copy(out=dst, in_=src)

        def quantise_x(a, e):
            stage, codes, scale = group_tiles[a, e]
            nc.vector.quantize_mx(out=codes[:].bitcast(FP8X4), scales=scale[:], in_=stage[:])

        gated = place([P, S], F32, "gated")
        windows = {engine: place([P, T], F32, "window_" + engine) for engine in ("scalar", "vector")}
        for window in windows.values():
            nc.vector.memset(window[:], 0.0)
        result = [place([P, T // 2], F32, "result%d" % n) for n in range(2)]

        def expert(e):
            for a in range(PASSES):
                nc.tensor.matmul_mx(
                    out=sum_bank(e)[:, 0, :],
                    lhsT=w_codes[e, a].bitcast(FP8X4),
                    lhsT_scale=w_scale[:, e * PASSES + a, :],
                    rhs=x_codes[a, e].bitcast(FP8X4),
                    rhs_scale=x_scale[a, e],
                    start=(a == 0),
                    stop=(a == PASSES - 1),
                )

        def bias_and_gate(e):
            tile, first = gate_tiles[e]
            nc.vector.scalar_tensor_tensor(
                gated[:, columns(e)], sum_bank(e)[:, 0, :], bias[:, e : e + 1], tile[:, (e - first) * C : (e - first + 1) * C], ADD, MULT
            )

        def scatter(engine, first, last):
            slots = offsets[:, first // PER_COLUMN : last // PER_COLUMN]
            if engine == "vector":
                nc.vector.tensor_copy(out=windows[engine][:].indirect(slots), in_=gated[:, first:last])
            else:
                nc.scalar.activation(windows[engine][:].indirect(slots), gated[:, first:last], COPY)

        round_pairs(0, 0, 0, slice(0, 528), "vector")
        round_pairs(0, 0, 0, slice(528, T), "scalar")
        gather(0, 0)
        round_pairs(0, 1, 0, slice(0, 320), "gpsimd")
        round_pairs(0, 1, 0, slice(320, T), "scalar")
        gather(0, 1)
        round_pairs(1, 0, 0, slice(0, 320), "gpsimd")
        round_pairs(1, 0, 0, slice(320, T), "scalar")
        gather(1, 0)
        interleave(0, LATE, "scalar")
        round_pairs(1, 1, 0, slice(0, 432), "gpsimd")
        round_pairs(1, 1, 0, slice(432, T), "scalar")
        gather(1, 1)
        interleave(0, EARLY, "scalar")
        quantise_u(0, EARLY, slice(0, 256))
        for n in range(WARM_UP):
            nc.tensor.matmul_mx(
                out=banks[7][:, :2, :].rearrange("p r s -> p (r s)"),
                lhsT=u_codes[0, 0][:, :P].bitcast(FP8X4),
                lhsT_scale=u_scale[0, 0][:, :P],
                rhs=u_codes[0, 0][:, : 2 * P].bitcast(FP8X4),
                rhs_scale=u_scale[0, 0][:, : 2 * P],
                start=True,
                stop=True,
            )
        interleave(1, EARLY, "vector")
        quantise_u(0, EARLY, slice(256, 512))
        round_wu(0, 0, HIGH, PAIRS[1], "gpsimd")
        round_wu(0, 0, slice(0, P), PAIRS[0], "scalar")
        round_wu(0, 0, LOW, PAIRS[1], "scalar")
        for rs in PAIRS:
            quantise_wu(0, 0, rs, slice(0, 2 * P))
        quantise_u(1, EARLY, slice(0, 512))
        for e in range(4):
            project(0, e, 0)
        for rs in PAIRS:
            round_wu(1, 0, slice(0, 32), rs, "vector")
            round_wu(1, 0, slice(32, P), rs, "scalar")
        for rs in PAIRS:
            quantise_wu(1, 0, rs, slice(0, 2 * P))
        for e in range(4):
            project(0, e, 1)
        interleave(1, LATE, "scalar")
        for g in range(PASSES):
            quantise_u(g, LATE, slice(0, 256))
        for e in range(4, E):
            for g in range(PASSES):
                project(0, e, g)
        for rs in PAIRS:
            round_wu(0, 1, slice(0, 48), rs, "vector")
            round_wu(0, 1, slice(48, P), rs, "scalar")
        for rs in PAIRS:
            quantise_wu(0, 1, rs, slice(0, 2 * P))
        for e in range(E - 1):
            empty(0, e)
        for e in range(AHEAD):
            project(1, e, 0)
        for ms in (LOW, HIGH):
            for rs in PAIRS:
                round_wu(1, 1, ms, rs, "vector")
            for rs in PAIRS:
                for r in range(2):
                    quantise_wu(1, 1, rs, slice(r * P + ms.start, r * P + ms.stop))
        quantise_x(0, 3)
        empty(0, E - 1)
        for e in range(E - 1):
            if e >= AHEAD:
                project(1, e, 0)
            project(1, e, 1)
            empty(1, e)
        quantise_x(0, 4)
        for e in range(2):
            quantise_x(1, e)
            expert(e)
        for g in range(PASSES):
            project(1, E - 1, g)
        quantise_x(0, 5)
        for e in range(2):
            bias_and_gate(e)
        scatter(*SCATTERS[0])
        for e in range(2, E):
            if e == E - 2:
                empty(1, E - 1)
            quantise_x(1, e)
            expert(e)
        for e in range(2, E):
            bias_and_gate(e)
        scatter(*SCATTERS[2])
        scatter(*SCATTERS[1])
        for n in range(2):
            half = slice(n * T // 2, (n + 1) * T // 2)
            nc.vector.tensor_tensor(result[n][:], windows["scalar"][:, half], windows["vector"][:, half], ADD)
            nc.sync.dma_start(out=out[:, half], in_=result[n][:])
